import numpy as np, ml_dtypes
CORES = [1,5,17,21,33,37,49,53]
N = 8
BF = ml_dtypes.bfloat16
def gentries(a):
    return np.ascontiguousarray(a.reshape(8, 16, -1).transpose(0, 2, 1)).reshape(8, -1)
def gtable(e):
    e = np.asarray(e); return np.ascontiguousarray(e.reshape(8, -1, 16).transpose(0, 2, 1)).reshape(128, -1).astype(np.int32)
def f(rng, *shape):
    return (rng.standard_normal(shape, dtype=np.float32) * np.exp2(rng.integers(-2, 3, shape[:-1] + (1,)))).astype(BF)
def wide(rng, *shape):
    v = f(rng, *shape).astype(np.float32); k = shape[:-2] + (1, shape[-1])
    return (v * np.exp2(rng.integers(-6, 7, k)) * (rng.random(k) > 0.0625)).astype(BF)
V, W, G, P, Q, RO = 3072, 2048, 128, 256, 96, 3
M = V + (N - 1) * G + 1
def nodes(an, of):
    A = np.full((N, 8, M), M - 1, np.int64); A[..., :V] = an
    O = np.zeros((N, 8, M), np.int64); O[..., :M - 1] = of
    return A, O
def dates(A, O):
    s, p = O, A
    for i in range(3):
        s = s + np.take_along_axis(s, p, 2); p = np.take_along_axis(p, p, 2)
    return s & (W - 1)
def parts(rng):
    u = rng.random((N, 8, V))
    an = np.where(u < 0.25, M - 1, np.where(u < 0.4, rng.integers(V, M - 1, (N, 8, V)), rng.integers(0, V, (N, 8, V))))
    return an, rng.integers(0, W, (N, 8, M - 1)), rng.integers(0, 256, (N, 8, 16, W)), rng.integers(0, V, (N, 8, (N - 1) * G))
def statures(rng):
    sc = np.exp2(rng.integers(-2, 3, (1, 8, 16, 1)).astype(np.float64)); sh = rng.choice(np.array([-0.8, -0.5, -0.2, 0.1]), (N, 8, 1, 1))
    x = rng.standard_normal((N, 8, 16, V)) + 0.7 * rng.standard_normal((N, 8, 1, V)) + sh
    s = rng.standard_normal((N, 8, 16, W)) + 0.7 * rng.standard_normal((N, 8, 1, W))
    return np.floor(8 * x) * 0.125 * sc, np.floor(8 * s) * 0.125 * sc
def pack(x, an, of, s, wk, snd):
    b = lambda v: np.ascontiguousarray(v).reshape(N, 128, -1).astype(np.float32).astype(BF)
    return {"x": b(x), "an0": np.stack([gtable(e) for e in an]), "of0": np.stack([gtable(e) for e in of]), "s0": b(s), "wk": b(wk), "snd": np.stack([gtable(e) for e in snd])}
def setup_inputs(rng):
    an, of, wk, snd = parts(rng); x, s = statures(rng)
    return pack(x, an, of, s, wk, snd)
def setup_inputs_room(rng):
    an, of, wk, snd = parts(rng); day = np.arange(W)
    an[..., 0] = M - 1; an[..., V - 1] = M - 1; of[..., 0] = 0; of[..., V - 1] = W - 2
    D = dates(*nodes(an, of))[..., :V]
    s = rng.integers(36, 61, (N, 8, 16, W)) * 0.25
    s[..., day % 4 == 3] = rng.integers(4, 29, (N, 8, 16, W // 4)) * 0.25
    o = s[1::2]; o[..., day % 4 == 1] = rng.integers(-32, -3, (o.shape[0], 8, 16, W // 4)) * 0.25
    k = rng.permutation(16)
    wk[:, :, k[0]] = 4 * rng.integers(0, 64, (N, 8, W)) + (day + 1) % 4
    wk[1::2, :, k[1]] = 4 * rng.integers(0, 64, (o.shape[0], 8, W)) + (day + 3) % 4
    x = 16 + rng.integers(0, 33, (N, 8, 16, V)) * 0.25
    for q in range(N):
        for g in range(8):
            n = int(rng.choice(np.array([0, 1, 2, P - 1, P, P + 1, P + Q]))); nf = int(rng.choice(np.array([0, 1, Q - 1, Q, Q + 1, P])))
            if q == 0: n = (P, P + 1, P - 1, 1, 0, P, P, P)[g]; nf = (Q, Q + 1, Q - 1, 1, 0, 0, P, Q + 1)[g]
            e = np.flatnonzero(D[q, g] % 2 == 0); e = e[(e > 0) & (e < V - 1)]
            w = np.concatenate([np.array([0, V - 1]), rng.permutation(e)])[:n]
            x[q, g][:, w] = rng.integers(29, 36, (16, len(w))) * 0.25
            i = w[len(w) - min(nf, len(w)):]
            x[q, g][:, i] = rng.integers(0, 4, (16, len(i))) * 0.25
    return pack(x, an, of, s, wk, snd)
def setup_inputs_ties(rng):
    an, of, wk, snd = parts(rng)
    of = rng.choice(np.array([0, 1, W - 1, W // 2, 14]), (N, 8, M - 1)); wk[:, ::2] = rng.choice(np.array([0, 1, 2, 255]), (N, 4, 16, W))
    x = np.floor(4 * rng.random((N, 8, 16, V)) * (0.3 + 0.7 * rng.random((N, 8, 1, V))))
    s = np.floor(4 * rng.random((N, 8, 16, W)) * (0.3 + 0.7 * rng.random((N, 8, 1, W)))) + 2 * (rng.random((N, 8, 1, W)) < 0.4)
    x[..., 0] = -1; x[..., V - 1] = -1
    x = np.where((x == 0) & (rng.random(x.shape) < 0.5), -0.0, x); s = np.where((s == 0) & (rng.random(s.shape) < 0.5), -0.0, s)
    return pack(x, an, of, s, wk, snd)
def setup_inputs_chains(rng):
    an, of, wk, snd = parts(rng); x, s = statures(rng); v = np.arange(V); d = int(rng.integers(0, W))
    for q in range(N):
        for g in range(8):
            k = (g + q) % 8
            if k == 0: an[q, g] = (v + 1) % V
            if k == 1: an[q, g] = v
            if k == 2: an[q, g] = rng.integers(V, M - 1, V)
            if k == 3: an[q, g] = M - 1
            if k == 4: an[q, g] = rng.choice(np.array([0, 5, V - 1]), V)
            if k == 5: an[q, g] = np.where(v == 0, M - 1, v - 1)
            if k > 5:
                an[q, g] = M - 1; of[q, g, :V] = d
                w = 1 + rng.permutation(255)[:16]; wk[q, g, :, d] = w; c = (d + 7 * w) & (W - 1)
                i = np.sort(rng.permutation(16)[:2])
                s[q, g] = 16 + 0.25 * rng.integers(0, 32, (16, W))
                s[q, g][:, c[i[0]]] = 0.25 * rng.integers(0, 16, 16)
                m = np.arange(P) if k == 6 else np.arange(int(rng.integers(0, 16)), V, 16)
                y = 28 + 0.25 * rng.integers(0, 16, (16, V))
                y[:, m] = 8 + 0.25 * rng.integers(0, 16, (16, len(m)))
                if k == 6: y[:, rng.permutation(P)[:56]] = -8 + 0.25 * rng.integers(0, 16, (16, 56))
                if k == 7: s[q, g][:, c[i[1]]] = -16 + 0.25 * rng.integers(0, 16, 16)
                x[q, g] = y
    snd[:, ::2] = rng.choice(np.array([0, 3, V // 2, V - 1]), (N, 4, (N - 1) * G))
    return pack(x, an, of, s, wk, snd)
def setup_inputs_calm(rng):
    an, of, wk, snd = parts(rng); x, s = statures(rng); q = int(rng.integers(0, N)); g = int(rng.integers(0, 8))
    x[:, g] += 64
    x[(q + 2) % N] += 64; x[q] = np.minimum(x[q], 20) - 64
    o = s[(q + 1) % N]; o[..., 1::2] -= 128
    w = rng.permutation(256)[:16]; wk[:, g, :, 0] = w; day = (7 * w) & (W - 1)
    for r in range(N):
        if r != q: s[r, g][:, day] = -2.0 ** 20
    x[q, :, :, 0] = -2.0 ** 20
    return pack(x, an, of, s, wk, snd)
def setup_inputs_spread(rng):
    an, of, wk, snd = parts(rng)
    of = np.minimum(np.exp2(13 * rng.random((N, 8, M - 1))).astype(np.int64) - 1, W - 1)
    x = np.abs(wide(rng, N, 8, 16, V).astype(np.float32)); s = np.abs(wide(rng, N, 8, 16, W).astype(np.float32))
    k = rng.permutation(8); sc = np.ones((1, 8, 1, 1), np.float32); sc[:, k[0]] = 2.0 ** -40; sc[:, k[1]] = 512
    x = np.minimum(x * sc, np.float32(2.0 ** 20)); s = np.minimum(s * sc, np.float32(2.0 ** 20))
    x[:, k[1], :, V - 1] = 2.0 ** 20; s[:, k[1], :, W - 1] = 2.0 ** 20
    return pack(x, an, of, s, wk, snd)
def check_inputs(d):
    bad = []
    for k, lo, hi in (("x", -2 ** 20, 2 ** 20), ("s0", -2 ** 20, 2 ** 20), ("wk", 0, 255), ("an0", 0, M - 1), ("of0", 0, W - 1), ("snd", 0, V - 1)):
        v = np.asarray(d[k]).astype(np.float64)
        if not (np.min(v) >= lo and np.max(v) <= hi): bad.append("range of " + k)
        elif k == "wk" and np.any(v != np.floor(v)): bad.append("whole numbers of wk")
        elif k in ("x", "s0") and np.any((v != 0) & (np.abs(v) < 2.0 ** -100)): bad.append("tiny numbers of " + k)
    return bad
def best(S, K, x, D):
    c = (D + 7 * K[:, D]) & (W - 1)
    e = np.sum((x[:, None, :] > S[:, c]).astype(np.int64), axis=0)
    k = np.argmax(e, axis=0); i = np.arange(len(D))
    return c[k, i], e[k, i]
def put(S, c, x):
    u, i = np.unique(c, return_index=True)
    S[:, u] = x[:, i]
def reference(x, an0, of0, s0, wk, snd):
    X = x.astype(np.float32).reshape(N, 8, 16, V); S = s0.astype(np.float32).reshape(N, 8, 16, W).copy(); K = wk.astype(np.float32).astype(np.int64).reshape(N, 8, 16, W)
    A, O = nodes(np.stack([gentries(e) for e in an0]).astype(np.int64), np.stack([gentries(e) for e in of0]).astype(np.int64))
    sl = np.stack([gentries(e) for e in snd]).astype(np.int64).reshape(N, 8, N - 1, G)
    odd = np.zeros(N, np.int64)
    for t in range(RO):
        D = dates(A, O)[..., :V]
        a = np.sum((X >= np.take_along_axis(S, D[:, :, None, :], 3)).astype(np.int64), axis=2)
        moves = np.zeros(N, np.int64); go = {}
        for q in range(N):
            for g in range(8):
                v = np.flatnonzero(a[q, g] < 5)[:P]
                c, e = best(S[q, g], K[q, g], X[q, g][:, v], D[q, g, v])
                ok = e >= 9 + odd[q]; w = v[ok]
                A[q, g, w] = M - 1; O[q, g, w] = c[ok]
                put(S[q, g], c[ok], X[q, g][:, w])
                moves[q] += len(w)
                r = v[~ok][:Q]; go[q, g] = (X[q, g][:, r], D[q, g, r])
        for q in range(N):
            for g in range(8):
                y, b = go[(q - 1 - t % (N - 1)) % N, g]
                c, e = best(S[q, g], K[q, g], y, b)
                ok = e >= 9 + odd[q]
                put(S[q, g], c[ok], y[:, ok])
        odd = moves & 1
        for q in range(N):
            for d in range(1, N):
                p = (q - d) % N
                O[q, :, V + (d - 1) * G:V + d * G] = np.take_along_axis(D[p], sl[p, :, d - 1], 1)
    return {"ys": S.reshape(N, 128, W).astype(BF), "yan": A[..., :V].astype(np.float32), "yof": O[..., :V].astype(np.float32)}

@@ -1,0 +1,686 @@
+from concourse.mybir import AluOpType as A, AxisListType, ActivationFunctionType as F
+
+V, W, NG, Q, RO = 3072, 2048, 896, 96, 3
+ROOT, BWW = 3968, 3984
+NEG = -4194304.0
+SC = 32768.0
+TINY = 2.0 ** -120
+bf, f3, i3, u1, fh = "bfloat16", "float32", "int32", "uint16", "float16"
+SCRATCH = {}
+
+
+def _sb(dt_, **kw):
+    for n, w in kw.items():
+        SCRATCH[n] = ("sbuf", [128] + (w if isinstance(w, list) else [w]), dt_)
+
+
+_sb(i3, anL=192, ofL=248, snL=56, tA=192, tB=248, tE=248, DI=192, DL=192, dg1=192, dg2=192, posI=192, loI=192, hiI=192,
+    ci=256, cm=256, key=496, smi=96, cpi=4, crow=128, crq=128, crg=128, c8=8, kri=256, kr2=256, j16=16)
+_sb(bf, pl0=248, pl1=248, pl2=248, pl3=248, XR=3968, XW=3088, SWIN=2304, WK=2048, BW=4240, PW1=BWW, PW2=V, SW1=BWW, SW2=BWW, G2=3088, GW=V,
+    BWc=V, SW1c=V,
+    dh=192, dlo=192, bits=V, SG=512, bT=192, binc=192, lob=192, hib=192, sq=192, OHL=V, OHH=V, indA=256, indB=256, ov=240,
+    xB=256, G2g=256, Dg=256, XX=4096, XXg=1536, B2=[16, 256], wkg=256, smb=80, RD=256, DE=[16, 256], DMb=[16, 16], dupR=256,
+    XP=2048, XS=2048, XE=2048, XLh=2048, XLl=2048, SA=2048, BD=128, BDt=128, M1=128, M1g=128, ID=128, NI=128, I7=128, CB=128, ONE=256,
+    ZER=256, OC=40, krow=256, KC=256, MK=[16, 16], GL0=NG, GL1=NG, GO0=NG, GO1=NG, GS0=544, GS1=544, GS2=544, GX0=192, GX1=192, GX2=192)
+_sb(f3, vf=16, sml=256, thr=3, ccol=64, BG=8, BA=8, tr=64)
+_sb(u1, SL=56, PL=192, PL1=192, PL2=192, DU=192, cu=256, smu=80)
+_sb(fh, ctc=[16, 32], ctt=[16, 32], cmh=16, cR=256, XA=2048, Ie=128, Io=128)
+SCRATCH["OUT"] = ("sbuf", [40, V], f3)
+for _b in range(8):
+    SCRATCH["ps%d" % _b] = ("psum", [128, 512], f3)
+SEMAPHORES = ["sv", "ss", "sp", "sg", "loc", "gh0", "gh1", "gu0", "gu1", "gu2"] + ["d%d" % k for k in range(60)]
+
+
+def rank_program(g, core, T, topo):
+    r = T.rank_of(core)
+    if r is None:
+        return
+    cores = T.cores
+    N = len(cores)
+    ENG = {"v": g.vector, "s": g.scalar, "p": g.tensor, "g": g, "y": g.sync}
+    SEM = {"v": "sv", "s": "ss", "p": "sp", "g": "sg"}
+    cnt = {"v": 0, "s": 0, "p": 0, "g": 0}
+    seen = {e: {} for e in ENG}
+    know = {}
+    tags = {}
+    total = {}
+
+    def tag(t):
+        if t not in tags:
+            tags[t] = {"w": [], "a": [], "r": []}
+        return tags[t]
+
+    def waits(e, deps):
+        m = {}
+        for sem, val in deps:
+            if seen[e].get(sem, 0) < val:
+                m[sem] = max(m.get(sem, 0), val)
+        for sem, val in list(m.items()):
+            for s2, v2 in m.items():
+                if s2 != sem and know.get((s2, v2), {}).get(sem, 0) >= val:
+                    m[sem] = 0
+        for sem, val in m.items():
+            if val:
+                ENG[e].wait_ge(T.sem[sem], val)
+            for s2, v2 in know.get((sem, val), {}).items():
+                seen[e][s2] = max(seen[e].get(s2, 0), v2)
+            seen[e][sem] = max(seen[e].get(sem, 0), val)
+
+    def deps_of(e, rd, wr, ap):
+        def some(x):
+            return [(s, n) for s, n, q in x if not (q == "p" and e == "p")]
+        d = []
+        for t in rd:
+            x = tag(t)
+            d += some(x["w"] + x["a"])
+            if t[:2] == "ps":
+                d += [(s, n) for s, n, q in x["r"] if q != e]
+        for t in wr:
+            x = tag(t)
+            d += some(x["w"] + x["a"] + x["r"])
+        for t in ap:
+            x = tag(t)
+            if x["r"]:
+                x["w"] = x["r"]; x["a"] = []; x["r"] = []
+            d += some(x["w"])
+        return d
+
+    def note(me, rd, wr, ap):
+        for t in rd:
+            tag(t)["r"].append(me)
+        for t in wr:
+            x = tag(t); x["w"] = [me]; x["a"] = []; x["r"] = []
+        for t in ap:
+            tag(t)["a"].append(me)
+
+    def op(e, fn, rd=(), wr=(), ap=()):
+        waits(e, deps_of(e, rd, wr, ap))
+        cnt[e] += 1
+        fn(ENG[e]).then_inc(T.sem[SEM[e]], 1)
+        know[(SEM[e], cnt[e])] = dict(seen[e])
+        total[SEM[e]] = cnt[e]
+        note((SEM[e], cnt[e], e), rd, wr, ap)
+
+    nd = [0]
+
+    def dma(out, in_, rd=(), wr=(), ap=()):
+        waits("y", deps_of("dma", rd, wr, ap))
+        s = "d%d" % nd[0]; nd[0] += 1
+        g.sync.dma_start(out, in_).then_inc(T.sem[s], 16)
+        know[(s, 16)] = dict(seen["y"])
+        total[s] = 16
+        note((s, 16, "dma"), rd, wr, ap)
+
+    def engs(src, dst):
+        return topo.engines(src, dst)[:8]
+
+    def arrive(sem, n, t):
+        total[sem] = n
+        tag(t)["w"].append((sem, n, "rem"))
+
+    def send(out, in_, dst, sem, rd):
+        waits("g", deps_of("rem", rd, (), ()))
+        rid, pid, _ = topo.addr(dst)
+        e = engs(core, dst)
+        m = 0
+        for k in e:
+            m |= 1 << k
+        g.remote_dma(out, in_, T.sem[sem], T.sem.loc, pid, rid, m)
+        total["loc"] = total.get("loc", 0) + len(e)
+
+    def ts(out, in0, s1, op0, rd, wr=(), ap=(), s2=None, op1=None):
+        if op1 is None:
+            op("v", lambda q: q.tensor_scalar(out, in0, s1, None, op0), rd, wr, ap)
+        else:
+            op("v", lambda q: q.tensor_scalar(out, in0, s1, s2, op0, op1), rd, wr, ap)
+
+    def tt(out, a, b, o, rd, wr=(), ap=()):
+        op("v", lambda q: q.tensor_tensor(out, a, b, o), rd, wr, ap)
+
+    def cp(out, in_, rd, wr=(), ap=()):
+        op("v", lambda q: q.tensor_copy(out, in_), rd, wr, ap)
+
+    def ms(out, c, wr=(), ap=()):
+        op("v", lambda q: q.memset(out, c), (), wr, ap)
+
+    def act(out, in_, rd, wr=(), ap=(), f=F.Copy, **kw):
+        op("s", lambda q: q.activation(out, in_, f, **kw), rd, wr, ap)
+
+    def mm(out, l, rh, st, sp, rd, wr=(), ap=()):
+        op("p", lambda q: q.matmul(out, l, rh, st, sp), rd, wr, ap)
+
+    def iota(out, pat, base, cm, wr):
+        op("g", lambda q: q.iota(out, pat, base, cm), (), wr)
+
+    def sl(i):
+        return slice(i * 128, (i + 1) * 128)
+
+    f_ = lambda k, nj: T.sml[:, 16 * k:16 * k + nj]
+    n_ = lambda k, nj: T.smi[:, 16 * k:16 * k + nj]
+    b_ = lambda k, nj: T.smb[:, 16 * k:16 * k + nj]
+    u_ = lambda k, nj: T.smu[:, 16 * k:16 * k + nj]
+    tr = lambda k, nj: T.tr[:, 16 * k:16 * k + nj]
+
+    dma(T.anL[:], T.an0[:], (), ["anL"])
+    dma(T.ofL[:], T.of0[:], (), ["ofL"])
+    dma(T.snL[:], T.snd[:], (), ["snL"])
+    dma(T.SWIN[:, 0:W], T.s0[:], (), ["S"])
+    dma(T.XW[:, 0:V], T.x[:], (), ["XWx"])
+    dma(T.WK[:], T.wk[:], (), ["WK"])
+    iota(T.cpi[:, 0:1], [[1, 1]], 0, 1, ["cpi"])
+    iota(T.c8[:], [[1, 8]], 0, 0, ["c8"])
+    iota(T.crow[:], [[1, 128]], 0, 0, ["crow"])
+    iota(T.j16[:], [[16, 16]], 0, 0, ["j16"])
+    iota(T.kri[:], [[1, 256]], 0, 0, ["kri"])
+    for n in ("SA", "XE", "XLh", "XLl"):
+        op("g", lambda q, n=n: q.iota(T[n][:], [[0, 2048]], 0, 0, allow_small_or_imprecise_dtypes=True), (), [n])
+    ms(T.XR[:], 0.0, ["XR"])
+
+    def col(k):
+        return T.ccol[:, k:k + 1]
+
+    ts(T.cpi[:, 1:2], T.cpi[:, 0:1], 15, A.bitwise_and, ["cpi"], ["cpi1"])
+    ts(T.cpi[:, 2:3], T.cpi[:, 0:1], 4, A.arith_shift_right, ["cpi"], ["cpi2"])
+    ts(T.cpi[:, 3:4], T.cpi[:, 0:1], 7, A.bitwise_and, ["cpi"], ["cpi3"])
+    cp(col(0), T.cpi[:, 0:1], ["cpi"], ["c0"])
+    cp(col(1), T.cpi[:, 1:2], ["cpi1"], ["c1"])
+    cp(col(2), T.cpi[:, 2:3], ["cpi2"], ["c2"])
+    cp(col(8), T.cpi[:, 3:4], ["cpi3"], ["c8c"])
+    ts(col(9), col(1), 0.0, A.is_equal, ["c1"], ["c9"], s2=256.0, op1=A.mult)
+    ts(col(10), col(1), 1.0, A.is_equal, ["c1"], ["c10"])
+    ts(T.BG[:], T.c8[:], col(2), A.is_equal, ["c8", "c2"], ["BG"])
+    tt(col(3), col(9), col(10), A.add, ["c9", "c10"], ["c3"])
+    ts(col(11), col(1), 2.0, A.is_equal, ["c1"], ["c11"], s2=32.0, op1=A.mult)
+    ts(col(12), col(1), 3.0, A.is_equal, ["c1"], ["c12"])
+    ts(col(15), col(1), 2.0, A.is_equal, ["c1"], ["c15"], s2=-252.0, op1=A.mult)
+    ts(col(13), col(9), 15.0 / 256.0, A.mult, ["c9"], ["c13"])
+    ts(col(14), col(10), 128.0, A.mult, ["c10"], ["c14"])
+    tt(col(4), col(11), col(12), A.add, ["c11", "c12"], ["c4"])
+    tt(col(5), col(13), col(14), A.add, ["c13", "c14"], ["c5"])
+    ms(T.pl0[:, 192:248], 15.0, ["pl0g"]); ms(T.pl1[:, 192:248], 128.0, ["pl1g"])
+    ts(T.tA[:], T.anL[:], 8, A.arith_shift_right, ["anL"], ["tA"])
+    ts(T.tB[:, 0:192], T.anL[:], 255, A.bitwise_and, ["anL"], ["tB"])
+    cp(T.pl0[:, 0:192], T.tA[:], ["tA"], ["pl0"])
+    cp(T.pl1[:, 0:192], T.tB[:, 0:192], ["tB"], ["pl1"])
+    dma(T.XR[0::16, :], T.pl0[:], ["pl0", "pl0g"], (), ["XR"])
+    dma(T.XR[1::16, :], T.pl1[:], ["pl1", "pl1g"], (), ["XR"])
+    ts(T.tB[:], T.ofL[:], 5, A.arith_shift_right, ["ofL"], ["tB"])
+    ts(T.tE[:], T.ofL[:], 31, A.bitwise_and, ["ofL"], ["tE"])
+    cp(T.pl2[:], T.tB[:], ["tB"], ["pl2"])
+    cp(T.pl3[:], T.tE[:], ["tE"], ["pl3"])
+    dma(T.XR[2::16, :], T.pl2[:], ["pl2"], (), ["XR"])
+    dma(T.XR[3::16, :], T.pl3[:], ["pl3"], (), ["XR"])
+    cp(T.PL[:], T.anL[:], ["anL"], ["PL"])
+    ms(T.ZER[:], 0.0, ["ZER"])
+    ms(T.PW1[:, V:BWW], 0.0, ["PW1g"])
+    ms(T.XP[:], 0.0, ["XP"]); ms(T.XS[:], 0.0, ["XS"])
+    ts(T.PW1[:, V:BWW], T.PW1[:, V:BWW], col(5), A.add, ["PW1g", "c5"], ["PW1g"])
+    for b in ("BW", "SW1", "SW2"):
+        ts(T[b][:, ROOT:BWW], T.ZER[:, 0:16], col(5), A.add, ["ZER", "c5"], [b + "r"])
+
+    def fill(n, src, rd, scale, o=None):
+        for i in range(16):
+            act(T[n][:, i * 128 + (i if o is None else o):(i + 1) * 128:16], T[src][:], [src] + rd, (), [n], scale=col(16 + i) if scale is None else scale)
+
+    fill("XP", "BG", ["c3"], col(3))
+    fill("XS", "BG", ["c4"], col(4))
+
+    def consts2():
+        ts(T.crq[:], T.crow[:], 15, A.bitwise_and, ["crow"], ["crq"])
+        ts(T.crg[:], T.crow[:], 4, A.arith_shift_right, ["crow"], ["crg"])
+        ts(T.ID[:], T.crow[:], col(0), A.is_equal, ["crow", "c0"], ["ID"])
+        ts(T.BD[:], T.crg[:], col(2), A.is_equal, ["crg", "c2"], ["BD"])
+        ms(T.ONE[:], 1.0, ["ONE"])
+        ts(T.BDt[:], T.crow[:], col(0), A.is_gt, ["crow", "c0"], ["BDt"], s2=-1.0, op1=A.add)
+        ts(T.M1[:], T.ID[:], -4096.0, A.mult, ["ID"], ["M1"])
+        ts(T.NI[:], T.ID[:], -1.0, A.mult, ["ID"], ["NI"])
+        tt(T.M1[:], T.M1[:], T.BDt[:], A.add, ["M1", "BDt"], ["M1"])
+        ms(T.thr[:, 0:1], 9 * SC, ["thr0"])
+        ts(T.XW[:, V:V + 16], T.ZER[:, 0:16], NEG, A.add, ["ZER"], ["XWp"])
+        cp(T.G2[:, V:V + 16], T.ZER[:, 0:16], ["ZER"], ["G2p"])
+        cp(T.krow[:], T.kri[:], ["kri"], ["krow"])
+        ts(T.BA[:], T.c8[:], col(8), A.is_equal, ["c8", "c8c"], ["BA"], s2=128.0, op1=A.mult)
+
+    def consts3():
+        for t in range(RO):
+            ms(T["GS%d" % t][:, 0:96], NEG, ["GSa%d" % t]); ms(T["GS%d" % t][:, 96:192], 0.0, ["GSb%d" % t])
+        ts(T.GW[:], T.XR[:, 0:V], 0.0, A.mult, ["XR", "c5"], ["GW"], s2=col(5), op1=A.add)
+        a, b = T.dg1[:, 0:56], T.dg2[:, 0:56]
+        ts(a, T.snL[:], 15, A.bitwise_and, ["snL"], ["dg1"])
+        ts(b, T.snL[:], 4, A.arith_shift_right, ["snL"], ["dg2"])
+        ts(a, a, 192.0, A.mult, ["dg1"], ["dg1"])
+        tt(a, a, b, A.add, ["dg1", "dg2"], ["dg1"])
+        cp(T.SL[:], a, ["dg1"], ["SL"])
+
+    def consts4():
+        ts(T.I7[:], T.ID[:], 7.0, A.mult, ["ID"], ["I7"])
+        ts(T.CB[:], T.BD[:], col(4), A.mult, ["BD", "c4"], ["CB"])
+        ts(T.cpi[:, 3:4], T.cpi[:, 2:3], 1, A.bitwise_and, ["cpi2", "c8c"], ["cpi3"])
+        ts(tr(0, 16), T.j16[:], col(1), A.add, ["j16", "c1"], ["kL"])
+        ts(T.kr2[:], T.kri[:], 15, A.bitwise_and, ["kri"], ["kr2"])
+        cp(col(7), T.cpi[:, 3:4], ["cpi3"], ["c7"])
+        ts(T.BDt[:], T.crq[:], col(1), A.is_gt, ["crq", "c1"], ["BDt"], s2=-1.0, op1=A.add)
+        ts(col(6), col(7), -1.0, A.mult, ["c7"], ["c6"], s2=1.0, op1=A.add)
+        ts(T.Io[:], T.ID[:], col(7), A.mult, ["ID", "c7"], ["Io"])
+        ts(T.Ie[:], T.ID[:], col(6), A.mult, ["ID", "c6"], ["Ie"])
+        ts(tr(1, 16), tr(0, 16), float(BWW), A.add, ["kL"], ["trP"])
+        ts(tr(2, 16), tr(0, 16), float(W), A.add, ["kL"], ["trS"])
+        ts(tr(3, 16), tr(0, 16), 192.0, A.add, ["kL"], ["trR"])
+        ts(T.KC[:], T.kr2[:], -2048.0, A.mult, ["kr2"], ["KC"], s2=15 * 2048.0, op1=A.add)
+        ts(T.M1g[:], T.ID[:], -4096.0, A.mult, ["ID"], ["M1g"])
+        tt(T.BDt[:], T.BDt[:], T.BD[:], A.mult, ["BDt", "BD"], ["BDt"])
+        ts(T.ccol[:, 16:32], T.crow[:, 0:16], col(1), A.is_equal, ["crow", "c1"], ["c16"])
+        ts(T.MK[:], T.kr2[:], col(1), A.is_gt, ["kr2", "c1"], ["MK"])
+        tt(T.M1g[:], T.M1g[:], T.BDt[:], A.add, ["M1g", "BDt"], ["M1g"])
+
+    def consts5():
+        for i in range(16):
+            ts(T.XA[:, sl(i)], T.BD[:], col(16 + i), A.mult, ["BD", "c16"], (), ["XA"])
+        fill("XLh", "BG", ["c16"], None, 2)
+        fill("XLl", "BG", ["c16"], None, 3)
+        ms(T.OC[:], 0.0, ["OC"])
+        ts(T.OC[:, 0:8], T.BG[:], col(3), A.mult, ["BG", "c3", "OC"], (), ["OC"])
+        ts(T.OC[:, 32:40], T.BG[:], col(4), A.mult, ["BG", "c4", "OC"], (), ["OC"])
+
+    consts2()
+    for i in range(16):
+        o, x = T.BW[:, i:ROOT:16], T.XR[:, i * 248:(i + 1) * 248]
+        if i % 4 < 3:
+            cp(o, x, ["XR"], (), ["BW"])
+        else:
+            act(o, x, ["XR"], (), ["BW"])
+
+    def keep():
+        for a in range(3):
+            f = slice(1024 * a, 1024 * (a + 1))
+            dma(T.BWc[:, f], T.BW[:, f], ["BW"], ["BWc%d" % a])
+
+    keep()
+    for b in ("SW1", "SW2"):
+        dma(T[b][:, V:ROOT], T.BW[:, V:ROOT], ["BW"], [b + "g"])
+
+    def ext(X, src, bank, c0, c1, st, sp, rd):
+        for i in range(16):
+            mm(T[bank][:, c0:c1], T[X][:, sl(i)], T[src][:, 16 * c0 + i:16 * c1:16], st and i == 0, sp and i == 15, [X] + rd, (), [bank])
+
+    BWT = ["BW", "BWg", "BWr"]
+    PT = ["PW10", "PW11", "PW12", "PW1g"]
+    S1T = ["SW10", "SW11", "SW12", "SW1g", "SW1r"]
+    S2T = ["SW20", "SW21", "SW22", "SW2g", "SW2r"]
+    DB = ["ps1", "ps3", "ps4"]
+
+    def th(a):
+        return slice(1024 * a, 1024 * (a + 1)), slice(64 * a, 64 * a + 64)
+
+    def L1s(a):
+        f, c = th(a)
+        act(T.PW1[:, f], T.BW[:, 0:BWW].indirect(T.PL[:, c]), BWT + ["PL"], ["PW1%d" % a])
+        ext("XP", "PW1", "ps0", 64 * a, 64 * a + 64, True, True, ["PW1%d" % a])
+
+    def L1v(a):
+        f, c = th(a)
+        tt(T.SW1[:, f], T.BW[:, 0:BWW].indirect(T.PL[:, c]), T.BWc[:, f], A.add, BWT + ["PL", "BWc%d" % a], ["SW1%d" % a])
+        dma(T.SW1c[:, f], T.SW1[:, f], ["SW1%d" % a], ["SW1c%d" % a])
+
+    def L2s(a):
+        f, c = th(a)
+        act(T.PW2[:, f], T.PW1[:, 0:BWW].indirect(T.PL1[:, c]), PT + ["PL1"], ["PW2%d" % a])
+        ext("XP", "PW2", "ps0", 64 * a, 64 * a + 64, True, True, ["PW2%d" % a])
+
+    def L2v(a):
+        f, c = th(a)
+        tt(T.SW2[:, f], T.SW1[:, 0:BWW].indirect(T.PL1[:, c]), T.SW1c[:, f], A.add, S1T + ["PL1", "SW1c%d" % a], ["SW2%d" % a])
+
+    def anchors(n):
+        cp(T[n][:], T.ps0[:, 0:192], ["ps0"], [n])
+
+    def L3a():
+        for a in range(3):
+            ext("XS", "SW2", DB[a], 64 * a, 64 * a + 64, True, False, [S2T[a]])
+        for a in range(3):
+            f, c = th(a)
+            if a < 2:
+                act(T.G2[:, f], T.SW2[:, 0:BWW].indirect(T.PL2[:, c]), S2T + ["PL2"], ["G2%d" % a])
+            else:
+                cp(T.G2[:, f], T.SW2[:, 0:BWW].indirect(T.PL2[:, c]), S2T + ["PL2"], ["G2%d" % a])
+
+    def L3e():
+        for a in range(3):
+            ext("XS", "G2", DB[a], 64 * a, 64 * a + 64, False, True, ["G2%d" % a])
+
+    def L3b():
+        for a in range(3):
+            cp(T.DI[:, th(a)[1]], T[DB[a]][:, th(a)[1]], [DB[a]], (), ["DI"])
+
+    def L3c():
+        ts(T.DL[:], T.DI[:], 2047, A.bitwise_and, ["DI"], ["DL"])
+        cp(T.DU[:], T.DL[:], ["DL"], ["DU"])
+
+    def beaten():
+        def counts(c0, c1, bt):
+            for c in range(c0, c1):
+                mm(T.ps2[:, 8 * c:8 * c + 8], T.bits[:, sl(c)], T.BD[:, 0::16], True, True, [bt, "BD"], (), ["ps2"])
+
+        def vec(l, h, t):
+            tt(T.bits[:, l:h], T.SWIN[:, 0:W].indirect(T.DU[:, l // 16:h // 16]), T.XW[:, l:h], A.is_le, ["S", "DU", "XWx"], [t])
+            counts(l // 128, h // 128, t)
+
+        act(T.SG[:], T.SWIN[:, 0:W].indirect(T.DU[:, 160:192]), ["S", "DU"], ["SG"])
+        vec(0, 1024, "bits0")
+        mm(T.ps7[:, :], T.ID[:], T.XW[:, 2560:3072], True, False, ["ID", "XWx"], ["ps7"])
+        mm(T.ps7[:, :], T.NI[:], T.SG[:], False, True, ["NI", "SG"], (), ["ps7"])
+        act(T.bits[:, 2560:3072], T.ps7[:, :], ["ps7"], ["bits3"], f=F.Sign, bias=TINY)
+        vec(1024, 2048, "bits1")
+        counts(20, 24, "bits3")
+        vec(2048, 2560, "bits2")
+        ts(T.bT[:, 0:160], T.ps2[:, 0:160], 4.5, A.is_lt, ["ps2"], ["bT"])
+        ts(T.bT[:, 160:192], T.ps2[:, 160:192], -7.0, A.is_lt, ["ps2"], (), ["bT"])
+
+    def ghosts_a():
+        ts(T.dg2[:], T.DL[:], 31, A.bitwise_and, ["DL"], ["dg2"])
+        ts(T.dg1[:], T.DL[:], 5, A.arith_shift_right, ["DL"], ["dg1"])
+        cp(T.dlo[:], T.dg2[:], ["dg2"], ["dlo"])
+        cp(T.dh[:], T.dg1[:], ["dg1"], ["dh"])
+        dma(T.GW[3::16, :], T.dlo[:], ["dlo"], (), ["GW"])
+        dma(T.GW[2::16, :], T.dh[:], ["dh"], (), ["GW"])
+
+    def ghosts_b(t):
+        act(T["GO%d" % t][:], T.GW[:].indirect(T.SL[:]), ["GW", "SL"], ["GO%d" % t])
+        for d in range(1, N):
+            send(T["GL%d" % t][:, sl(d - 1)], T["GO%d" % t][:, sl(d - 1)], cores[(r + d) % N], "gh%d" % t, ["GO%d" % t])
+        arrive("gh%d" % t, sum(len(engs(cores[(r - d) % N], core)) for d in range(1, N)), "GL%d" % t)
+
+    def ghosts_in(t):
+        for b in ("BW", "SW1", "SW2"):
+            dma(T[b][:, V:ROOT], T["GL%d" % t][:], ["GL%d" % t], [b + "g"])
+
+    NS = 6
+    vU = u_(4, 16)
+    DUm = lambda nj: u_(3, nj)
+
+    def compact(t):
+        mm(T.ps3[:, 0:192], T.M1[:], T.bT[:], True, False, ["M1", "bT"], ["ps3"])
+        for c in range(8):
+            op("v", lambda q, c=c: q.tensor_tensor_scan(T.binc[:, c::8], T.ONE[:, c:192:8], T.bT[:, c::8], 0.0, A.mult, A.add),
+               ["ONE", "bT"], (), ["binc"])
+        mm(T.ps3[:, 0:192], T.ONE[:, 0:128], T.binc[:], False, True, ["ONE", "binc"], (), ["ps3"])
+        mm(T.ps4[:, 0:1], T.binc[:, 0:128], T.ONE[:, 0:1], True, True, ["binc", "ONE"], ["ps4"])
+        mm(T.ps4[0:64, 1:2], T.binc[:, 128:192], T.ONE[:, 0:1], True, True, ["binc", "ONE"], (), ["ps4"])
+        ts(T.posI[:], T.ps3[:, 0:192], 4095.0, A.add, ["ps3"], ["posI"])
+        ts(T.indA[:], T.krow[:], T.ps4[:, 0:1], A.is_ge, ["krow", "ps4"], ["indA"])
+        ts(T.loI[:], T.posI[:], 15, A.bitwise_and, ["posI"], ["loI"])
+        ts(T.hiI[:], T.posI[:], 4, A.arith_shift_right, ["posI"], ["hiI"])
+        ts(T.indB[0:64, :], T.krow[0:64, :], T.ps4[0:64, 1:2], A.is_ge, ["krow", "ps4"], ["indB"])
+        cp(T.lob[:], T.loI[:], ["loI"], ["lob"])
+        cp(T.hib[:], T.hiI[:], ["hiI"], ["hib"])
+        for i in range(16):
+            mm(T.ps6[:, 0:16], T.SA[:, sl(i)], T.indA[:, i::16], i == 0, False, ["SA", "indA"], (), ["ps6"])
+        for i in range(16):
+            mm(T.ps6[:, 0:16], T.SA[0:64, sl(i)], T.indB[0:64, i::16], False, i == 15, ["SA", "indB"], (), ["ps6"])
+        for i in range(NS):
+            act(T.sq[:], T.lob[:], ["lob"], ["sq"], f=F.Square, bias=-float(i))
+            act(T.OHL[:, i::16], T.sq[:], ["sq"], (), ["OHL"], f=F.Relu, scale=-1.0, bias=1.0)
+        if t < RO - 1:
+            ghosts_b(t)
+        for i in range(NS, 16):
+            ts(T.OHL[:, i::16], T.lob[:], float(i), A.is_equal, ["lob"], (), ["OHL"])
+        for i in range(16):
+            ts(T.OHH[:, i::16], T.hib[:], float(i), A.is_equal, ["hib", "c0"], (), ["OHH"], s2=col(0), op1=A.mult)
+        for c in range(24):
+            mm(T.ps5[:, 0:128], T.OHL[:, sl(c)], T.OHH[:, sl(c)], c == 0, c == 23, ["OHL", "OHH"], (), ["ps5"])
+        if t == 0:
+            consts5()
+        o = lambda a, b: T.ov[:, a:b]
+        tt(o(0, 128), T.ps5[:, 0:128], T.BD[:], A.mult, ["ps5", "BD"], ["ovm"])
+        tt(o(128, 192), o(0, 64), o(64, 128), A.add, ["ovm"], ["ov1"])
+        tt(o(192, 224), o(128, 160), o(160, 192), A.add, ["ov1"], ["ov2"])
+        tt(o(224, 240), o(192, 208), o(208, 224), A.add, ["ov2"], ["ov3"])
+        tt(T.vf[:], T.ps6[:, 0:16], o(224, 240), A.add, ["ps6", "ov3"], ["vf"])
+        cp(vU, T.vf[:], ["vf"], ["vU"])
+
+    def own_data():
+        act(T.G2g[:], T.G2[:].indirect(vU), ["G20", "G21", "G22", "G2p", "vU", "c15"], ["G2g"], f=F.Identity, bias=col(15))
+        cp(T.xB[:], T.XW[:].indirect(vU), ["XWx", "XWp", "vU"], ["xB"])
+        tt(T.Dg[:], T.SW2[:, 0:BWW].indirect(vU), T.G2g[:], A.add, S2T + ["G2g", "vU"], ["Dg"])
+
+    def spread(x, xt, XX, n, ks, e):
+        for k in ks:
+            if e == "v":
+                cp(T[XX][:, k:16 * n:16], x, [xt], (), [XX])
+            else:
+                act(T[XX][:, k:16 * n:16], x, [xt], (), [XX])
+
+    def choose_a(Dg, dt_, nj):
+        for i in range(16):
+            mm(T.ps6[:, 0:nj], T.XS[:, sl(i)], Dg[:, i::16], i == 0, i == 15, ["XS", dt_], (), ["ps6"])
+        mm(T.ps7[:, 0:16 * nj], T.CB[:], Dg, True, False, ["CB", dt_], ["ps7"])
+
+    def choose_b(nj):
+        n = 16 * nj
+        ts(n_(4, nj), T.ps6[:, 0:nj], 8064.0, A.add, ["ps6"], ["di"])
+        ts(n_(5, nj), n_(4, nj), 2047, A.bitwise_and, ["di"], ["dm"])
+        cp(DUm(nj), n_(5, nj), ["dm"], ["DUm"])
+        cp(T.wkg[:, 0:n], T.WK[:].indirect(DUm(nj)), ["WK", "DUm"], ["wkg"])
+        mm(T.ps7[:, 0:n], T.I7[:], T.wkg[:, 0:n], False, True, ["I7", "wkg"], (), ["ps7"])
+
+    def choose_c(nj):
+        n = 16 * nj
+        ts(T.ci[:, 0:n], T.ps7[:, 0:n], 8064.0, A.add, ["ps7"], ["ci"])
+        ts(T.cm[:, 0:n], T.ci[:, 0:n], 2047, A.bitwise_and, ["ci"], ["cm"])
+        cp(T.cu[:, 0:n], T.cm[:, 0:n], ["cm"], ["cu"])
+
+    def choose_d(XX, nj, parts):
+        n = 16 * nj
+        mm(T.ps2[:, 0:n], T.ID[:], T.KC[:, 0:n], True, False, ["ID", "KC"], ["ps2"])
+        for j0, j1 in parts:
+            for j in range(j0, j1):
+                tt(T.B2[:, j, :], T.SWIN[:, 0:W].indirect(T.cu[:, 16 * j:16 * j + 16]), T[XX][:, 256 * j:256 * j + 256], A.is_lt,
+                   ["S", "cu", XX], ["B2%d" % j])
+            for i in range(16):
+                mm(T.ps2[:, 16 * j0:16 * j1], T.XE[:, sl(i)], T.B2[:, j0:j1, 16 * i:16 * i + 16], False, False,
+                   ["XE"] + ["B2%d" % j for j in range(j0, j1)], (), ["ps2"])
+        cp(T.ctc[:, 0:nj, 0:16], T.cm[:, 0:n], ["cm"], (), ["ctc"])
+        cp(T.ctc[:, 0:nj, 16:32], T.cm[:, 0:n], ["cm"], (), ["ctc"])
+        op("v", lambda q: q.transpose(T.ctt[:, 0:nj, :], T.ctc[:, 0:nj, :]), ["ctc"], ["ctt"])
+        mm(T.ps2[:, 0:n], T.Ie[:], T.ctt[:, 0:nj, 0:16], False, False, ["Ie", "ctt"], (), ["ps2"])
+        mm(T.ps2[:, 0:n], T.Io[:], T.ctt[:, 0:nj, 16:32], False, True, ["Io", "ctt"], (), ["ps2"])
+
+    def choose_e(nj):
+        n = 16 * nj
+        K = T.key
+        cp(K[:, 0:n], T.ps2[:, 0:n], ["ps2"], ["key0"])
+        tt(K[:, 256:256 + n // 2], K[:, 0:n:2], K[:, 1:n:2], A.max, ["key0"], ["key1"])
+        tt(K[:, 384:384 + n // 4], K[:, 256:256 + n // 2:2], K[:, 257:256 + n // 2:2], A.max, ["key1"], ["key2"])
+        tt(K[:, 448:448 + n // 8], K[:, 384:384 + n // 4:2], K[:, 385:384 + n // 4:2], A.max, ["key2"], ["key3"])
+        tt(K[:, 480:480 + nj], K[:, 448:448 + n // 8:2], K[:, 449:448 + n // 8:2], A.max, ["key3"], ["kmax"])
+
+    def moved(t, nj):
+        km = T.key[:, 480:480 + nj]
+        ts(f_(0, nj), km, T.thr[:, t:t + 1], A.is_ge, ["kmax", "thr%d" % t], ["mv"])
+        ts(n_(0, nj), km, 2047, A.bitwise_and, ["kmax"], ["c1i"])
+
+    def early():
+        tt(f_(14, 16), T.vf[:], tr(1, 16), A.subtract, ["vf", "trP"], ["vt"])
+        ts(f_(15, 16), T.vf[:], 3071.5, A.is_lt, ["vf"], ["val"])
+
+    def move_list():
+        km = T.key[:, 480:496]
+        ts(n_(3, 16), km, 31, A.bitwise_and, ["kmax"], ["c4i"])
+        ts(n_(2, 16), km, 5, A.arith_shift_right, ["kmax"], ["c3i"], s2=63, op1=A.bitwise_and)
+        cp(b_(1, 16), n_(3, 16), ["c4i"], ["lb"])
+        cp(b_(0, 16), n_(2, 16), ["c3i"], ["hb"])
+        for i in range(16):
+            mm(T.ps3[:, i:256:16], T.XLh[:, sl(i)], b_(0, 16), True, False, ["XLh", "hb"], (), ["ps3"])
+            mm(T.ps3[:, i:256:16], T.XLl[:, sl(i)], b_(1, 16), False, True, ["XLl", "lb"], (), ["ps3"])
+        act(T.RD[:], T.ps3[:, 0:256], ["ps3", "c5"], ["RD"], f=F.Identity, bias=col(5))
+        tt(f_(2, 16), f_(0, 16), f_(14, 16), A.mult, ["mv", "vt"], ["m1"])
+        tt(u_(0, 16), f_(2, 16), tr(1, 16), A.add, ["m1", "trP"], ["voff"])
+
+    def move_put(last):
+        cp(T.BW[:, 0:4240].indirect(u_(0, 16)), T.RD[:], ["RD", "voff"], BWT)
+        if not last:
+            keep()
+
+    def refuse_a():
+        tt(b_(2, 16), f_(15, 16), f_(0, 16), A.subtract, ["val", "mv"], ["rf"])
+        op("v", lambda q: q.tensor_tensor_scan(b_(3, 16), T.ONE[:, 0:16], b_(2, 16), 0.0, A.mult, A.add), ["ONE", "rf"], ["finc"])
+        mm(T.ps4[:, 0:16], T.M1g[:], b_(2, 16), True, False, ["M1g", "rf"], ["ps4"])
+        mm(T.ps4[:, 0:16], T.BD[:], b_(3, 16), False, True, ["BD", "finc"], (), ["ps4"])
+
+    def refuse_b():
+        ts(f_(3, 16), T.ps4[:, 0:16], 4095.0, A.add, ["ps4"], ["rq"])
+        ts(f_(4, 16), f_(3, 16), 95.5, A.is_lt, ["rq"], ["rs"])
+        tt(f_(5, 16), f_(3, 16), tr(3, 16), A.subtract, ["rq", "trR"], ["rt"])
+        tt(f_(6, 16), f_(4, 16), f_(5, 16), A.mult, ["rs", "rt"], ["rr"])
+        tt(u_(1, 16), f_(6, 16), tr(3, 16), A.add, ["rr", "trR"], ["roff"])
+
+    def refuse_c(t):
+        G = T["GS%d" % t]
+        ga, gb = "GSa%d" % t, "GSb%d" % t
+        cp(G[:, 0:448].indirect(u_(1, 16)), T.xB[:], ["xB", "roff"], [ga, gb])
+        cp(G[:, 96:544].indirect(u_(1, 16)), T.Dg[:], ["Dg", "roff", ga], [gb])
+        dst, src = cores[(r + 1 + t % (N - 1)) % N], cores[(r - 1 - t % (N - 1)) % N]
+        send(T["GX%d" % t][:], G[:, 0:192], dst, "gu%d" % t, [ga, gb])
+        arrive("gu%d" % t, len(engs(src, core)), "GX%d" % t)
+
+    def parity_a():
+        op("v", lambda q: q.tensor_reduce(f_(7, 1), f_(0, 16), AxisListType.X, A.add), ["mv"], ["mr"])
+        cp(b_(4, 1), f_(7, 1), ["mr"], ["mrb"])
+        mm(T.ps4[:, 16:17], T.ONE[:, 0:128], b_(4, 1), True, True, ["ONE", "mrb"], (), ["ps4"])
+
+    def parity_b(t):
+        cp(n_(1, 1), T.ps4[:, 16:17], ["ps4"], ["pi"])
+        ts(n_(1, 1), n_(1, 1), 1, A.bitwise_and, ["pi"], ["pi"])
+        ts(T.thr[:, t + 1:t + 2], n_(1, 1), SC, A.mult, ["pi"], ["thr%d" % (t + 1)], s2=9 * SC, op1=A.add)
+
+    def dedup_a(nj):
+        ts(f_(8, nj), n_(0, nj), 1.0, A.add, ["c1i"], ["cp1"])
+        tt(f_(10, nj), n_(0, nj), tr(2, nj), A.subtract, ["c1i", "trS"], ["ct2"])
+        tt(f_(9, nj), f_(8, nj), f_(0, nj), A.mult, ["cp1", "mv"], ["cmf"])
+        cp(T.cmh[:, 0:nj], f_(9, nj), ["cmf"], ["cmh"])
+        for i in range(16):
+            mm(T.ps5[:, i:16 * nj:16], T.XA[:, sl(i)], T.cmh[:, 0:nj], True, True, ["XA", "cmh"], (), ["ps5"])
+
+    def dedup_b(nj):
+        n = 16 * nj
+        cp(T.cR[:, 0:n], T.ps5[:, 0:n], ["ps5"], ["cR"])
+        mm(T.ps5[:, 0:n], T.BD[:], T.ZER[:, 0:n], True, False, ["BD", "ZER"], ["ps5"])
+        for j in range(nj):
+            ts(T.DE[:, j, 0:n - 16 * j], T.cR[:, 16 * j:n], T.sml[:, 144 + j:145 + j], A.is_equal, ["cR", "cmf"], ["DE%d" % j])
+            if j < nj - 1:
+                mm(T.ps5[:, 16 * (j + 1):n], T.BD[:], T.DE[:, j, 16:n - 16 * j], False, False, ["BD", "DE%d" % j], (), ["ps5"])
+        tt(T.DMb[:, 0:nj, :], T.DE[:, 0:nj, 0:16], T.MK[:, 0:nj, :], A.mult, ["DE%d" % j for j in range(nj)] + ["MK"], ["DMb"])
+        mm(T.ps5[:, 0:n], T.BD[:], T.DMb[:, 0:nj, :], False, True, ["BD", "DMb"], (), ["ps5"])
+
+    def dedup_c(nj):
+        n = 16 * nj
+        cp(T.dupR[:, 0:n], T.ps5[:, 0:n], ["ps5"], ["dupR"])
+        for i in range(16):
+            mm(T.ps6[:, 16:16 + nj], T.XE[:, sl(i)], T.dupR[:, i:n:16], i == 0, i == 15, ["XE", "dupR"], (), ["ps6"])
+
+    def dedup_d(nj, x, xt):
+        ts(f_(11, nj), T.ps6[:, 16:16 + nj], 0.5, A.is_lt, ["ps6"], ["nd"])
+        tt(f_(12, nj), f_(11, nj), f_(0, nj), A.mult, ["nd", "mv"], ["fm"])
+        tt(f_(13, nj), f_(12, nj), f_(10, nj), A.mult, ["fm", "ct2"], ["fq"])
+        tt(u_(2, nj), f_(13, nj), tr(2, nj), A.add, ["fq", "trS"], ["soff"])
+        cp(T.SWIN[:, 0:2304].indirect(u_(2, nj)), x, [xt, "soff"], ["S"])
+
+    for t in range(RO):
+        last = t == RO - 1
+        if t:
+            gx, gt = T["GX%d" % (t - 1)], "GX%d" % (t - 1)
+            ghosts_in(t - 1)
+            ext("XP", "BW", "ps0", 0, 192, True, True, ["BW"])
+            dedup_b(16)
+            anchors("PL")
+        for a in range(3):
+            L1s(a)
+        L1v(0)
+        if t:
+            dedup_c(16)
+        L1v(1); L1v(2)
+        anchors("PL1")
+        for a in range(3):
+            L2s(a)
+        if t:
+            dedup_d(16, T.xB[:], "xB")
+            choose_a(gx[:, 96:192], gt, 6)
+            spread(gx[:, 0:96], gt, "XXg", Q, range(16), "v")
+        L2v(0)
+        if t == 0:
+            fill("SA", "BA", [], 1.0)
+        else:
+            choose_b(6)
+        L2v(1)
+        anchors("PL2")
+        L2v(2)
+        L3a()
+        if t == 0:
+            consts3(); consts4()
+            fill("XE", "BG", [], SC)
+        else:
+            choose_c(6)
+            choose_d("XXg", 6, [(0, 6)])
+            choose_e(6); moved(t - 1, 6); dedup_a(6)
+        L3e()
+        if t:
+            dedup_b(6)
+        L3b()
+        if t:
+            dedup_c(6)
+        L3c()
+        if t:
+            dedup_d(6, gx[:, 0:96], gt)
+        beaten()
+        if not last:
+            ghosts_a()
+        compact(t)
+        own_data()
+        spread(T.xB[:], "xB", "XX", 256, range(0, 9), "s")
+        choose_a(T.Dg[:], "Dg", 16)
+        spread(T.xB[:], "xB", "XX", 256, range(9, 16), "v")
+        early()
+        choose_b(16)
+        choose_c(16)
+        choose_d("XX", 16, [(0, 4), (4, 8), (8, 12), (12, 16)])
+        choose_e(16)
+        moved(t, 16)
+        refuse_a()
+        if last:
+            dedup_a(16)
+            refuse_b(); refuse_c(t)
+        else:
+            move_list()
+            refuse_b()
+            dedup_a(16)
+            parity_a()
+            refuse_c(t)
+            move_put(False)
+            parity_b(t)
+    gx, gt = T.GX2, "GX2"
+    dedup_b(16); dedup_c(16)
+    move_list()
+    dedup_d(16, T.xB[:], "xB")
+    spread(gx[:, 0:96], gt, "XXg", Q, range(16), "v")
+    choose_a(gx[:, 96:192], gt, 6)
+    choose_b(6); choose_c(6)
+    choose_d("XXg", 6, [(0, 6)])
+    move_put(True)
+    choose_e(6); moved(2, 6); dedup_a(6)
+
+    def outs(b):
+        p = ["ps0", "ps1", "ps3"][b % 3]
+        mm(T[p][0:40, :], T.OC[:], T.BW[:, 512 * b:512 * b + 512], True, True, ["OC", "BW"], [p])
+        act(T.OUT[:, 512 * b:512 * b + 512], T[p][0:40, :], [p], (), ["OUT"])
+
+    dedup_b(6)
+    for b in range(2):
+        outs(b)
+    dedup_c(6); dedup_d(6, gx[:, 0:96], gt)
+    for b in range(2, 6):
+        outs(b)
+    dma(T.yan[:], T.OUT[0:8, :], ["OUT"])
+    dma(T.yof[:], T.OUT[32:40, :], ["OUT"])
+    dma(T.ys[:], T.SWIN[:, 0:W], ["S"])
+    for s in total:
+        g.wait_ge(T.sem[s], total[s])

@@ -16,8 +16,8 @@ def _sb(dt_, **kw):
 
 _sb(i3, anL=192, ofL=248, snL=56, tA=192, tB=248, tE=248, DI=192, DL=192, dg1=192, dg2=192, posI=192, loI=192, hiI=192,
     ci=256, cm=256, key=496, smi=96, cpi=4, crow=128, crq=128, crg=128, c8=8, kri=256, kr2=256, j16=16)
-_sb(bf, pl0=248, pl1=248, pl2=248, pl3=248, XR=3968, XW=3088, SWIN=2304, WK=2048, BW=4240, PW1=BWW, PW2=V, SW1=BWW, SW2=BWW, G2=3088, GW=V,
-    BWc=V, SW1c=V,
+_sb(bf, pl0=248, pl1=248, pl2=248, pl3=248, XR=3968, XW=3088, SWIN=2304, WK=2048, BW=4240, SW1=BWW, SW2=BWW, G2=3088, GW=V,
+    Zb=V, Zs=V,
     dh=192, dlo=192, bits=V, SG=512, bT=192, binc=192, lob=192, hib=192, sq=192, OHL=V, OHH=V, indA=256, indB=256, ov=240,
     xB=256, G2g=256, Dg=256, XX=4096, XXg=1536, B2=[16, 256], wkg=256, smb=80, RD=256, DE=[16, 256], DMb=[16, 16], dupR=256,
     XP=2048, XS=2048, XE=2048, XLh=2048, XLl=2048, SA=2048, BD=128, BDt=128, M1=128, M1g=128, ID=128, NI=128, I7=128, CB=128, ONE=256,
@@ -172,8 +172,8 @@ def rank_program(g, core, T, topo):
     iota(T.crow[:], [[1, 128]], 0, 0, ["crow"])
     iota(T.j16[:], [[16, 16]], 0, 0, ["j16"])
     iota(T.kri[:], [[1, 256]], 0, 0, ["kri"])
-    for n in ("SA", "XE", "XLh", "XLl"):
-        op("g", lambda q, n=n: q.iota(T[n][:], [[0, 2048]], 0, 0, allow_small_or_imprecise_dtypes=True), (), [n])
+    for n, w in (("Zb", V), ("Zs", V), ("SA", 2048), ("XE", 2048), ("XLh", 2048), ("XLl", 2048)):
+        op("g", lambda q, n=n, w=w: q.iota(T[n][:], [[0, w]], 0, 0, allow_small_or_imprecise_dtypes=True), (), [n])
     ms(T.XR[:], 0.0, ["XR"])
 
     def col(k):
@@ -191,7 +191,7 @@ def rank_program(g, core, T, topo):
     ts(T.BG[:], T.c8[:], col(2), A.is_equal, ["c8", "c2"], ["BG"])
     tt(col(3), col(9), col(10), A.add, ["c9", "c10"], ["c3"])
     ts(col(11), col(1), 2.0, A.is_equal, ["c1"], ["c11"], s2=32.0, op1=A.mult)
-    ts(col(12), col(1), 3.0, A.is_equal, ["c1"], ["c12"])
+    ts(col(12), col(1), 10.0, A.is_equal, ["c1"], ["c12"])
     ts(col(15), col(1), 2.0, A.is_equal, ["c1"], ["c15"], s2=-252.0, op1=A.mult)
     ts(col(13), col(9), 15.0 / 256.0, A.mult, ["c9"], ["c13"])
     ts(col(14), col(10), 128.0, A.mult, ["c10"], ["c14"])
@@ -209,12 +209,10 @@ def rank_program(g, core, T, topo):
     cp(T.pl2[:], T.tB[:], ["tB"], ["pl2"])
     cp(T.pl3[:], T.tE[:], ["tE"], ["pl3"])
     dma(T.XR[2::16, :], T.pl2[:], ["pl2"], (), ["XR"])
-    dma(T.XR[3::16, :], T.pl3[:], ["pl3"], (), ["XR"])
+    dma(T.XR[10::16, :], T.pl3[:], ["pl3"], (), ["XR"])
     cp(T.PL[:], T.anL[:], ["anL"], ["PL"])
     ms(T.ZER[:], 0.0, ["ZER"])
-    ms(T.PW1[:, V:BWW], 0.0, ["PW1g"])
     ms(T.XP[:], 0.0, ["XP"]); ms(T.XS[:], 0.0, ["XS"])
-    ts(T.PW1[:, V:BWW], T.PW1[:, V:BWW], col(5), A.add, ["PW1g", "c5"], ["PW1g"])
     for b in ("BW", "SW1", "SW2"):
         ts(T[b][:, ROOT:BWW], T.ZER[:, 0:16], col(5), A.add, ["ZER", "c5"], [b + "r"])
 
@@ -277,7 +275,7 @@ def rank_program(g, core, T, topo):
         for i in range(16):
             ts(T.XA[:, sl(i)], T.BD[:], col(16 + i), A.mult, ["BD", "c16"], (), ["XA"])
         fill("XLh", "BG", ["c16"], None, 2)
-        fill("XLl", "BG", ["c16"], None, 3)
+        fill("XLl", "BG", ["c16"], None, 10)
         ms(T.OC[:], 0.0, ["OC"])
         ts(T.OC[:, 0:8], T.BG[:], col(3), A.mult, ["BG", "c3", "OC"], (), ["OC"])
         ts(T.OC[:, 32:40], T.BG[:], col(4), A.mult, ["BG", "c4", "OC"], (), ["OC"])
@@ -290,59 +288,50 @@ def rank_program(g, core, T, topo):
         else:
             act(o, x, ["XR"], (), ["BW"])
 
+    def th(a):
+        return slice(1024 * a, 1024 * (a + 1)), slice(64 * a, 64 * a + 64)
+
     def keep():
         for a in range(3):
-            f = slice(1024 * a, 1024 * (a + 1))
-            dma(T.BWc[:, f], T.BW[:, f], ["BW"], ["BWc%d" % a])
+            f = th(a)[0]
+            dma(T.Zb[2::8, f], T.BW[2::8, f], ["BW", "Zb"], (), ["Zb%d" % a])
 
     keep()
     for b in ("SW1", "SW2"):
         dma(T[b][:, V:ROOT], T.BW[:, V:ROOT], ["BW"], [b + "g"])
+    consts4()
 
     def ext(X, src, bank, c0, c1, st, sp, rd):
         for i in range(16):
             mm(T[bank][:, c0:c1], T[X][:, sl(i)], T[src][:, 16 * c0 + i:16 * c1:16], st and i == 0, sp and i == 15, [X] + rd, (), [bank])
 
     BWT = ["BW", "BWg", "BWr"]
-    PT = ["PW10", "PW11", "PW12", "PW1g"]
     S1T = ["SW10", "SW11", "SW12", "SW1g", "SW1r"]
     S2T = ["SW20", "SW21", "SW22", "SW2g", "SW2r"]
     DB = ["ps1", "ps3", "ps4"]
+    LV = {1: ("BW", BWT, "PL", "Zb", "SW1"), 2: ("SW1", S1T, "PL1", "Zs", "SW2")}
 
-    def th(a):
-        return slice(1024 * a, 1024 * (a + 1)), slice(64 * a, 64 * a + 64)
-
-    def L1s(a):
+    def dbl(l, a):
+        w, wt, p, z, n = LV[l]
         f, c = th(a)
-        act(T.PW1[:, f], T.BW[:, 0:BWW].indirect(T.PL[:, c]), BWT + ["PL"], ["PW1%d" % a])
-        ext("XP", "PW1", "ps0", 64 * a, 64 * a + 64, True, True, ["PW1%d" % a])
-
-    def L1v(a):
-        f, c = th(a)
-        tt(T.SW1[:, f], T.BW[:, 0:BWW].indirect(T.PL[:, c]), T.BWc[:, f], A.add, BWT + ["PL", "BWc%d" % a], ["SW1%d" % a])
-        dma(T.SW1c[:, f], T.SW1[:, f], ["SW1%d" % a], ["SW1c%d" % a])
-
-    def L2s(a):
-        f, c = th(a)
-        act(T.PW2[:, f], T.PW1[:, 0:BWW].indirect(T.PL1[:, c]), PT + ["PL1"], ["PW2%d" % a])
-        ext("XP", "PW2", "ps0", 64 * a, 64 * a + 64, True, True, ["PW2%d" % a])
-
-    def L2v(a):
-        f, c = th(a)
-        tt(T.SW2[:, f], T.SW1[:, 0:BWW].indirect(T.PL1[:, c]), T.SW1c[:, f], A.add, S1T + ["PL1", "SW1c%d" % a], ["SW2%d" % a])
+        tt(T[n][:, f], T[w][:, 0:BWW].indirect(T[p][:, c]), T[z][:, f], A.add, wt + [p, z, z + str(a)], [n + str(a)])
+        ext("XP", n, "ps0", 64 * a, 64 * a + 64, True, True, [n + str(a)])
+        if l == 1:
+            dma(T.Zs[2::8, f], T.SW1[2::8, f], ["SW1%d" % a, "Zs"], (), ["Zs%d" % a])
 
     def anchors(n):
         cp(T[n][:], T.ps0[:, 0:192], ["ps0"], [n])
 
     def L3a():
         for a in range(3):
-            ext("XS", "SW2", DB[a], 64 * a, 64 * a + 64, True, False, [S2T[a]])
-        for a in range(3):
+            ext("XS", "SW2", DB[a], 64 * a, 64 * a + 64, True, False, S2T[:3])
+        for a in range(2):
             f, c = th(a)
-            if a < 2:
-                act(T.G2[:, f], T.SW2[:, 0:BWW].indirect(T.PL2[:, c]), S2T + ["PL2"], ["G2%d" % a])
-            else:
-                cp(T.G2[:, f], T.SW2[:, 0:BWW].indirect(T.PL2[:, c]), S2T + ["PL2"], ["G2%d" % a])
+            act(T.G2[:, f], T.SW2[:, 0:BWW].indirect(T.PL2[:, c]), S2T + ["PL2"], ["G2%d" % a])
+
+    def L3v():
+        f, c = th(2)
+        cp(T.G2[:, f], T.SW2[:, 0:BWW].indirect(T.PL2[:, c]), S2T + ["PL2"], ["G22"])
 
     def L3e():
         for a in range(3):
@@ -381,7 +370,7 @@ def rank_program(g, core, T, topo):
         ts(T.dg1[:], T.DL[:], 5, A.arith_shift_right, ["DL"], ["dg1"])
         cp(T.dlo[:], T.dg2[:], ["dg2"], ["dlo"])
         cp(T.dh[:], T.dg1[:], ["dg1"], ["dh"])
-        dma(T.GW[3::16, :], T.dlo[:], ["dlo"], (), ["GW"])
+        dma(T.GW[10::16, :], T.dlo[:], ["dlo"], (), ["GW"])
         dma(T.GW[2::16, :], T.dh[:], ["dh"], (), ["GW"])
 
     def ghosts_b(t):
@@ -394,7 +383,7 @@ def rank_program(g, core, T, topo):
         for b in ("BW", "SW1", "SW2"):
             dma(T[b][:, V:ROOT], T["GL%d" % t][:], ["GL%d" % t], [b + "g"])
 
-    NS = 6
+    NS = 7
     vU = u_(4, 16)
     DUm = lambda nj: u_(3, nj)
 
@@ -420,14 +409,14 @@ def rank_program(g, core, T, topo):
         for i in range(NS):
             act(T.sq[:], T.lob[:], ["lob"], ["sq"], f=F.Square, bias=-float(i))
             act(T.OHL[:, i::16], T.sq[:], ["sq"], (), ["OHL"], f=F.Relu, scale=-1.0, bias=1.0)
-        if t < RO - 1:
-            ghosts_b(t)
         for i in range(NS, 16):
             ts(T.OHL[:, i::16], T.lob[:], float(i), A.is_equal, ["lob"], (), ["OHL"])
         for i in range(16):
             ts(T.OHH[:, i::16], T.hib[:], float(i), A.is_equal, ["hib", "c0"], (), ["OHH"], s2=col(0), op1=A.mult)
         for c in range(24):
             mm(T.ps5[:, 0:128], T.OHL[:, sl(c)], T.OHH[:, sl(c)], c == 0, c == 23, ["OHL", "OHH"], (), ["ps5"])
+        if t < RO - 1:
+            ghosts_a()
         if t == 0:
             consts5()
         o = lambda a, b: T.ov[:, a:b]
@@ -450,14 +439,16 @@ def rank_program(g, core, T, topo):
             else:
                 act(T[XX][:, k:16 * n:16], x, [xt], (), [XX])
 
+    LB = {16: "ps6", 6: "ps4"}
+
     def choose_a(Dg, dt_, nj):
         for i in range(16):
-            mm(T.ps6[:, 0:nj], T.XS[:, sl(i)], Dg[:, i::16], i == 0, i == 15, ["XS", dt_], (), ["ps6"])
+            mm(T[LB[nj]][:, 0:nj], T.XS[:, sl(i)], Dg[:, i::16], i == 0, i == 15, ["XS", dt_], (), [LB[nj]])
         mm(T.ps7[:, 0:16 * nj], T.CB[:], Dg, True, False, ["CB", dt_], ["ps7"])
 
     def choose_b(nj):
         n = 16 * nj
-        ts(n_(4, nj), T.ps6[:, 0:nj], 8064.0, A.add, ["ps6"], ["di"])
+        ts(n_(4, nj), T[LB[nj]][:, 0:nj], 8064.0, A.add, [LB[nj]], ["di"])
         ts(n_(5, nj), n_(4, nj), 2047, A.bitwise_and, ["di"], ["dm"])
         cp(DUm(nj), n_(5, nj), ["dm"], ["DUm"])
         cp(T.wkg[:, 0:n], T.WK[:].indirect(DUm(nj)), ["WK", "DUm"], ["wkg"])
@@ -593,34 +584,33 @@ def rank_program(g, core, T, topo):
             ext("XP", "BW", "ps0", 0, 192, True, True, ["BW"])
             dedup_b(16)
             anchors("PL")
-        for a in range(3):
-            L1s(a)
-        L1v(0)
+        dbl(1, 0)
         if t:
             dedup_c(16)
-        L1v(1); L1v(2)
-        anchors("PL1")
-        for a in range(3):
-            L2s(a)
+        dbl(1, 1); dbl(1, 2)
         if t:
             dedup_d(16, T.xB[:], "xB")
+        anchors("PL1")
+        if t:
+            spread(gx[:, 0:96], gt, "XXg", Q, range(16), "s")
             choose_a(gx[:, 96:192], gt, 6)
-            spread(gx[:, 0:96], gt, "XXg", Q, range(16), "v")
-        L2v(0)
+        dbl(2, 0)
         if t == 0:
             fill("SA", "BA", [], 1.0)
         else:
             choose_b(6)
-        L2v(1)
+        dbl(2, 1); dbl(2, 2)
+        if t:
+            choose_c(6)
         anchors("PL2")
-        L2v(2)
         L3a()
         if t == 0:
-            consts3(); consts4()
+            consts3()
             fill("XE", "BG", [], SC)
+            L3v()
         else:
-            choose_c(6)
             choose_d("XXg", 6, [(0, 6)])
+            L3v()
             choose_e(6); moved(t - 1, 6); dedup_a(6)
         L3e()
         if t:
@@ -632,8 +622,6 @@ def rank_program(g, core, T, topo):
         if t:
             dedup_d(6, gx[:, 0:96], gt)
         beaten()
-        if not last:
-            ghosts_a()
         compact(t)
         own_data()
         spread(T.xB[:], "xB", "XX", 256, range(0, 9), "s")
@@ -641,6 +629,8 @@ def rank_program(g, core, T, topo):
         spread(T.xB[:], "xB", "XX", 256, range(9, 16), "v")
         early()
         choose_b(16)
+        if not last:
+            ghosts_b(t)
         choose_c(16)
         choose_d("XX", 16, [(0, 4), (4, 8), (8, 12), (12, 16)])
         choose_e(16)
@@ -659,11 +649,11 @@ def rank_program(g, core, T, topo):
             parity_b(t)
     gx, gt = T.GX2, "GX2"
     dedup_b(16); dedup_c(16)
-    move_list()
-    dedup_d(16, T.xB[:], "xB")
-    spread(gx[:, 0:96], gt, "XXg", Q, range(16), "v")
     choose_a(gx[:, 96:192], gt, 6)
+    spread(gx[:, 0:96], gt, "XXg", Q, range(16), "s")
+    dedup_d(16, T.xB[:], "xB")
     choose_b(6); choose_c(6)
+    move_list()
     choose_d("XXg", 6, [(0, 6)])
     move_put(True)
     choose_e(6); moved(2, 6); dedup_a(6)

from concourse.mybir import AluOpType as A, AxisListType, ActivationFunctionType as F

V, W, NG, Q, RO = 3072, 2048, 896, 96, 3
ROOT, BWW = 3968, 3984
NEG = -4194304.0
SC = 32768.0
TINY = 2.0 ** -120
bf, f3, i3, u1, fh = "bfloat16", "float32", "int32", "uint16", "float16"
SCRATCH = {}


def _sb(dt_, **kw):
    for n, w in kw.items():
        SCRATCH[n] = ("sbuf", [128] + (w if isinstance(w, list) else [w]), dt_)


_sb(i3, anL=192, ofL=248, snL=56, tA=192, tB=248, tE=248, DI=192, DL=192, dg1=192, dg2=192, posI=192, loI=192, hiI=192,
    ci=256, cm=256, key=496, smi=96, cpi=4, crow=128, crq=128, crg=128, c8=8, kri=256, kr2=256, j16=16)
_sb(bf, pl0=248, pl1=248, pl2=248, pl3=248, XR=3968, XW=3088, SWIN=2304, WK=2048, BW=4240, SW1=BWW, SW2=BWW, G2=3088, GW=V,
    Zb=V, Zs=V,
    dh=192, dlo=192, bits=V, SG=512, bT=192, binc=192, lob=192, hib=192, sq=192, OHL=V, OHH=V, indA=256, indB=256, ov=240,
    xB=256, G2g=256, Dg=256, XX=4096, XXg=1536, B2=[16, 256], wkg=256, smb=80, RD=256, DE=[16, 256], DMb=[16, 16], dupR=256,
    XP=2048, XS=2048, XE=2048, XLh=2048, XLl=2048, SA=2048, BD=128, BDt=128, M1=128, M1g=128, ID=128, NI=128, I7=128, CB=128, ONE=256,
    ZER=256, OC=40, krow=256, KC=256, MK=[16, 16], GL0=NG, GL1=NG, GO0=NG, GO1=NG, GS0=544, GS1=544, GS2=544, GX0=192, GX1=192, GX2=192)
_sb(f3, vf=16, sml=256, thr=3, ccol=64, BG=8, BA=8, tr=64)
_sb(u1, SL=56, PL=192, PL1=192, PL2=192, DU=192, cu=256, smu=80)
_sb(fh, ctc=[16, 32], ctt=[16, 32], cmh=16, cR=256, XA=2048, Ie=128, Io=128)
SCRATCH["OUT"] = ("sbuf", [40, V], f3)
for _b in range(8):
    SCRATCH["ps%d" % _b] = ("psum", [128, 512], f3)
SEMAPHORES = ["sv", "ss", "sp", "sg", "loc", "gh0", "gh1", "gu0", "gu1", "gu2"] + ["d%d" % k for k in range(60)]


def rank_program(g, core, T, topo):
    r = T.rank_of(core)
    if r is None:
        return
    cores = T.cores
    N = len(cores)
    ENG = {"v": g.vector, "s": g.scalar, "p": g.tensor, "g": g, "y": g.sync}
    SEM = {"v": "sv", "s": "ss", "p": "sp", "g": "sg"}
    cnt = {"v": 0, "s": 0, "p": 0, "g": 0}
    seen = {e: {} for e in ENG}
    know = {}
    tags = {}
    total = {}

    def tag(t):
        if t not in tags:
            tags[t] = {"w": [], "a": [], "r": []}
        return tags[t]

    def waits(e, deps):
        m = {}
        for sem, val in deps:
            if seen[e].get(sem, 0) < val:
                m[sem] = max(m.get(sem, 0), val)
        for sem, val in list(m.items()):
            for s2, v2 in m.items():
                if s2 != sem and know.get((s2, v2), {}).get(sem, 0) >= val:
                    m[sem] = 0
        for sem, val in m.items():
            if val:
                ENG[e].wait_ge(T.sem[sem], val)
            for s2, v2 in know.get((sem, val), {}).items():
                seen[e][s2] = max(seen[e].get(s2, 0), v2)
            seen[e][sem] = max(seen[e].get(sem, 0), val)

    def deps_of(e, rd, wr, ap):
        def some(x):
            return [(s, n) for s, n, q in x if not (q == "p" and e == "p")]
        d = []
        for t in rd:
            x = tag(t)
            d += some(x["w"] + x["a"])
            if t[:2] == "ps":
                d += [(s, n) for s, n, q in x["r"] if q != e]
        for t in wr:
            x = tag(t)
            d += some(x["w"] + x["a"] + x["r"])
        for t in ap:
            x = tag(t)
            if x["r"]:
                x["w"] = x["r"]; x["a"] = []; x["r"] = []
            d += some(x["w"])
        return d

    def note(me, rd, wr, ap):
        for t in rd:
            tag(t)["r"].append(me)
        for t in wr:
            x = tag(t); x["w"] = [me]; x["a"] = []; x["r"] = []
        for t in ap:
            tag(t)["a"].append(me)

    def op(e, fn, rd=(), wr=(), ap=()):
        waits(e, deps_of(e, rd, wr, ap))
        cnt[e] += 1
        fn(ENG[e]).then_inc(T.sem[SEM[e]], 1)
        know[(SEM[e], cnt[e])] = dict(seen[e])
        total[SEM[e]] = cnt[e]
        note((SEM[e], cnt[e], e), rd, wr, ap)

    nd = [0]

    def dma(out, in_, rd=(), wr=(), ap=()):
        waits("y", deps_of("dma", rd, wr, ap))
        s = "d%d" % nd[0]; nd[0] += 1
        g.sync.dma_start(out, in_).then_inc(T.sem[s], 16)
        know[(s, 16)] = dict(seen["y"])
        total[s] = 16
        note((s, 16, "dma"), rd, wr, ap)

    def engs(src, dst):
        return topo.engines(src, dst)[:8]

    def arrive(sem, n, t):
        total[sem] = n
        tag(t)["w"].append((sem, n, "rem"))

    def send(out, in_, dst, sem, rd):
        waits("g", deps_of("rem", rd, (), ()))
        rid, pid, _ = topo.addr(dst)
        e = engs(core, dst)
        m = 0
        for k in e:
            m |= 1 << k
        g.remote_dma(out, in_, T.sem[sem], T.sem.loc, pid, rid, m)
        total["loc"] = total.get("loc", 0) + len(e)

    def ts(out, in0, s1, op0, rd, wr=(), ap=(), s2=None, op1=None):
        if op1 is None:
            op("v", lambda q: q.tensor_scalar(out, in0, s1, None, op0), rd, wr, ap)
        else:
            op("v", lambda q: q.tensor_scalar(out, in0, s1, s2, op0, op1), rd, wr, ap)

    def tt(out, a, b, o, rd, wr=(), ap=()):
        op("v", lambda q: q.tensor_tensor(out, a, b, o), rd, wr, ap)

    def cp(out, in_, rd, wr=(), ap=()):
        op("v", lambda q: q.tensor_copy(out, in_), rd, wr, ap)

    def ms(out, c, wr=(), ap=()):
        op("v", lambda q: q.memset(out, c), (), wr, ap)

    def act(out, in_, rd, wr=(), ap=(), f=F.Copy, **kw):
        op("s", lambda q: q.activation(out, in_, f, **kw), rd, wr, ap)

    def mm(out, l, rh, st, sp, rd, wr=(), ap=()):
        op("p", lambda q: q.matmul(out, l, rh, st, sp), rd, wr, ap)

    def iota(out, pat, base, cm, wr):
        op("g", lambda q: q.iota(out, pat, base, cm), (), wr)

    def sl(i):
        return slice(i * 128, (i + 1) * 128)

    f_ = lambda k, nj: T.sml[:, 16 * k:16 * k + nj]
    n_ = lambda k, nj: T.smi[:, 16 * k:16 * k + nj]
    b_ = lambda k, nj: T.smb[:, 16 * k:16 * k + nj]
    u_ = lambda k, nj: T.smu[:, 16 * k:16 * k + nj]
    tr = lambda k, nj: T.tr[:, 16 * k:16 * k + nj]

    dma(T.anL[:], T.an0[:], (), ["anL"])
    dma(T.ofL[:], T.of0[:], (), ["ofL"])
    dma(T.snL[:], T.snd[:], (), ["snL"])
    dma(T.SWIN[:, 0:W], T.s0[:], (), ["S"])
    dma(T.XW[:, 0:V], T.x[:], (), ["XWx"])
    dma(T.WK[:], T.wk[:], (), ["WK"])
    iota(T.cpi[:, 0:1], [[1, 1]], 0, 1, ["cpi"])
    iota(T.c8[:], [[1, 8]], 0, 0, ["c8"])
    iota(T.crow[:], [[1, 128]], 0, 0, ["crow"])
    iota(T.j16[:], [[16, 16]], 0, 0, ["j16"])
    iota(T.kri[:], [[1, 256]], 0, 0, ["kri"])
    for n, w in (("Zb", V), ("Zs", V), ("SA", 2048), ("XE", 2048), ("XLh", 2048), ("XLl", 2048)):
        op("g", lambda q, n=n, w=w: q.iota(T[n][:], [[0, w]], 0, 0, allow_small_or_imprecise_dtypes=True), (), [n])
    ms(T.XR[:], 0.0, ["XR"])

    def col(k):
        return T.ccol[:, k:k + 1]

    ts(T.cpi[:, 1:2], T.cpi[:, 0:1], 15, A.bitwise_and, ["cpi"], ["cpi1"])
    ts(T.cpi[:, 2:3], T.cpi[:, 0:1], 4, A.arith_shift_right, ["cpi"], ["cpi2"])
    ts(T.cpi[:, 3:4], T.cpi[:, 0:1], 7, A.bitwise_and, ["cpi"], ["cpi3"])
    cp(col(0), T.cpi[:, 0:1], ["cpi"], ["c0"])
    cp(col(1), T.cpi[:, 1:2], ["cpi1"], ["c1"])
    cp(col(2), T.cpi[:, 2:3], ["cpi2"], ["c2"])
    cp(col(8), T.cpi[:, 3:4], ["cpi3"], ["c8c"])
    ts(col(9), col(1), 0.0, A.is_equal, ["c1"], ["c9"], s2=256.0, op1=A.mult)
    ts(col(10), col(1), 1.0, A.is_equal, ["c1"], ["c10"])
    ts(T.BG[:], T.c8[:], col(2), A.is_equal, ["c8", "c2"], ["BG"])
    tt(col(3), col(9), col(10), A.add, ["c9", "c10"], ["c3"])
    ts(col(11), col(1), 2.0, A.is_equal, ["c1"], ["c11"], s2=32.0, op1=A.mult)
    ts(col(12), col(1), 10.0, A.is_equal, ["c1"], ["c12"])
    ts(col(15), col(1), 2.0, A.is_equal, ["c1"], ["c15"], s2=-252.0, op1=A.mult)
    ts(col(13), col(9), 15.0 / 256.0, A.mult, ["c9"], ["c13"])
    ts(col(14), col(10), 128.0, A.mult, ["c10"], ["c14"])
    tt(col(4), col(11), col(12), A.add, ["c11", "c12"], ["c4"])
    tt(col(5), col(13), col(14), A.add, ["c13", "c14"], ["c5"])
    ms(T.pl0[:, 192:248], 15.0, ["pl0g"]); ms(T.pl1[:, 192:248], 128.0, ["pl1g"])
    ts(T.tA[:], T.anL[:], 8, A.arith_shift_right, ["anL"], ["tA"])
    ts(T.tB[:, 0:192], T.anL[:], 255, A.bitwise_and, ["anL"], ["tB"])
    cp(T.pl0[:, 0:192], T.tA[:], ["tA"], ["pl0"])
    cp(T.pl1[:, 0:192], T.tB[:, 0:192], ["tB"], ["pl1"])
    dma(T.XR[0::16, :], T.pl0[:], ["pl0", "pl0g"], (), ["XR"])
    dma(T.XR[1::16, :], T.pl1[:], ["pl1", "pl1g"], (), ["XR"])
    ts(T.tB[:], T.ofL[:], 5, A.arith_shift_right, ["ofL"], ["tB"])
    ts(T.tE[:], T.ofL[:], 31, A.bitwise_and, ["ofL"], ["tE"])
    cp(T.pl2[:], T.tB[:], ["tB"], ["pl2"])
    cp(T.pl3[:], T.tE[:], ["tE"], ["pl3"])
    dma(T.XR[2::16, :], T.pl2[:], ["pl2"], (), ["XR"])
    dma(T.XR[10::16, :], T.pl3[:], ["pl3"], (), ["XR"])
    cp(T.PL[:], T.anL[:], ["anL"], ["PL"])
    ms(T.ZER[:], 0.0, ["ZER"])
    ms(T.XP[:], 0.0, ["XP"]); ms(T.XS[:], 0.0, ["XS"])
    for b in ("BW", "SW1", "SW2"):
        ts(T[b][:, ROOT:BWW], T.ZER[:, 0:16], col(5), A.add, ["ZER", "c5"], [b + "r"])

    def fill(n, src, rd, scale, o=None):
        for i in range(16):
            act(T[n][:, i * 128 + (i if o is None else o):(i + 1) * 128:16], T[src][:], [src] + rd, (), [n], scale=col(16 + i) if scale is None else scale)

    fill("XP", "BG", ["c3"], col(3))
    fill("XS", "BG", ["c4"], col(4))

    def consts2():
        ts(T.crq[:], T.crow[:], 15, A.bitwise_and, ["crow"], ["crq"])
        ts(T.crg[:], T.crow[:], 4, A.arith_shift_right, ["crow"], ["crg"])
        ts(T.ID[:], T.crow[:], col(0), A.is_equal, ["crow", "c0"], ["ID"])
        ts(T.BD[:], T.crg[:], col(2), A.is_equal, ["crg", "c2"], ["BD"])
        ms(T.ONE[:], 1.0, ["ONE"])
        ts(T.BDt[:], T.crow[:], col(0), A.is_gt, ["crow", "c0"], ["BDt"], s2=-1.0, op1=A.add)
        ts(T.M1[:], T.ID[:], -4096.0, A.mult, ["ID"], ["M1"])
        ts(T.NI[:], T.ID[:], -1.0, A.mult, ["ID"], ["NI"])
        tt(T.M1[:], T.M1[:], T.BDt[:], A.add, ["M1", "BDt"], ["M1"])
        ms(T.thr[:, 0:1], 9 * SC, ["thr0"])
        ts(T.XW[:, V:V + 16], T.ZER[:, 0:16], NEG, A.add, ["ZER"], ["XWp"])
        cp(T.G2[:, V:V + 16], T.ZER[:, 0:16], ["ZER"], ["G2p"])
        cp(T.krow[:], T.kri[:], ["kri"], ["krow"])
        ts(T.BA[:], T.c8[:], col(8), A.is_equal, ["c8", "c8c"], ["BA"], s2=128.0, op1=A.mult)

    def consts3():
        for t in range(RO):
            ms(T["GS%d" % t][:, 0:96], NEG, ["GSa%d" % t]); ms(T["GS%d" % t][:, 96:192], 0.0, ["GSb%d" % t])
        ts(T.GW[:], T.XR[:, 0:V], 0.0, A.mult, ["XR", "c5"], ["GW"], s2=col(5), op1=A.add)
        a, b = T.dg1[:, 0:56], T.dg2[:, 0:56]
        ts(a, T.snL[:], 15, A.bitwise_and, ["snL"], ["dg1"])
        ts(b, T.snL[:], 4, A.arith_shift_right, ["snL"], ["dg2"])
        ts(a, a, 192.0, A.mult, ["dg1"], ["dg1"])
        tt(a, a, b, A.add, ["dg1", "dg2"], ["dg1"])
        cp(T.SL[:], a, ["dg1"], ["SL"])

    def consts4():
        ts(T.I7[:], T.ID[:], 7.0, A.mult, ["ID"], ["I7"])
        ts(T.CB[:], T.BD[:], col(4), A.mult, ["BD", "c4"], ["CB"])
        ts(T.cpi[:, 3:4], T.cpi[:, 2:3], 1, A.bitwise_and, ["cpi2", "c8c"], ["cpi3"])
        ts(tr(0, 16), T.j16[:], col(1), A.add, ["j16", "c1"], ["kL"])
        ts(T.kr2[:], T.kri[:], 15, A.bitwise_and, ["kri"], ["kr2"])
        cp(col(7), T.cpi[:, 3:4], ["cpi3"], ["c7"])
        ts(T.BDt[:], T.crq[:], col(1), A.is_gt, ["crq", "c1"], ["BDt"], s2=-1.0, op1=A.add)
        ts(col(6), col(7), -1.0, A.mult, ["c7"], ["c6"], s2=1.0, op1=A.add)
        ts(T.Io[:], T.ID[:], col(7), A.mult, ["ID", "c7"], ["Io"])
        ts(T.Ie[:], T.ID[:], col(6), A.mult, ["ID", "c6"], ["Ie"])
        ts(tr(1, 16), tr(0, 16), float(BWW), A.add, ["kL"], ["trP"])
        ts(tr(2, 16), tr(0, 16), float(W), A.add, ["kL"], ["trS"])
        ts(tr(3, 16), tr(0, 16), 192.0, A.add, ["kL"], ["trR"])
        ts(T.KC[:], T.kr2[:], -2048.0, A.mult, ["kr2"], ["KC"], s2=15 * 2048.0, op1=A.add)
        ts(T.M1g[:], T.ID[:], -4096.0, A.mult, ["ID"], ["M1g"])
        tt(T.BDt[:], T.BDt[:], T.BD[:], A.mult, ["BDt", "BD"], ["BDt"])
        ts(T.ccol[:, 16:32], T.crow[:, 0:16], col(1), A.is_equal, ["crow", "c1"], ["c16"])
        ts(T.MK[:], T.kr2[:], col(1), A.is_gt, ["kr2", "c1"], ["MK"])
        tt(T.M1g[:], T.M1g[:], T.BDt[:], A.add, ["M1g", "BDt"], ["M1g"])

    def consts5():
        for i in range(16):
            ts(T.XA[:, sl(i)], T.BD[:], col(16 + i), A.mult, ["BD", "c16"], (), ["XA"])
        fill("XLh", "BG", ["c16"], None, 2)
        fill("XLl", "BG", ["c16"], None, 10)
        ms(T.OC[:], 0.0, ["OC"])
        ts(T.OC[:, 0:8], T.BG[:], col(3), A.mult, ["BG", "c3", "OC"], (), ["OC"])
        ts(T.OC[:, 32:40], T.BG[:], col(4), A.mult, ["BG", "c4", "OC"], (), ["OC"])

    consts2()
    for i in range(16):
        o, x = T.BW[:, i:ROOT:16], T.XR[:, i * 248:(i + 1) * 248]
        if i % 4 < 3:
            cp(o, x, ["XR"], (), ["BW"])
        else:
            act(o, x, ["XR"], (), ["BW"])

    def th(a):
        return slice(1024 * a, 1024 * (a + 1)), slice(64 * a, 64 * a + 64)

    def keep():
        for a in range(3):
            f = th(a)[0]
            dma(T.Zb[2::8, f], T.BW[2::8, f], ["BW", "Zb"], (), ["Zb%d" % a])

    keep()
    for b in ("SW1", "SW2"):
        dma(T[b][:, V:ROOT], T.BW[:, V:ROOT], ["BW"], [b + "g"])
    consts4()

    def ext(X, src, bank, c0, c1, st, sp, rd):
        for i in range(16):
            mm(T[bank][:, c0:c1], T[X][:, sl(i)], T[src][:, 16 * c0 + i:16 * c1:16], st and i == 0, sp and i == 15, [X] + rd, (), [bank])

    BWT = ["BW", "BWg", "BWr"]
    S1T = ["SW10", "SW11", "SW12", "SW1g", "SW1r"]
    S2T = ["SW20", "SW21", "SW22", "SW2g", "SW2r"]
    DB = ["ps1", "ps3", "ps4"]
    LV = {1: ("BW", BWT, "PL", "Zb", "SW1"), 2: ("SW1", S1T, "PL1", "Zs", "SW2")}

    def dbl(l, a):
        w, wt, p, z, n = LV[l]
        f, c = th(a)
        tt(T[n][:, f], T[w][:, 0:BWW].indirect(T[p][:, c]), T[z][:, f], A.add, wt + [p, z, z + str(a)], [n + str(a)])
        ext("XP", n, "ps0", 64 * a, 64 * a + 64, True, True, [n + str(a)])
        if l == 1:
            dma(T.Zs[2::8, f], T.SW1[2::8, f], ["SW1%d" % a, "Zs"], (), ["Zs%d" % a])

    def anchors(n):
        cp(T[n][:], T.ps0[:, 0:192], ["ps0"], [n])

    def L3a():
        for a in range(3):
            ext("XS", "SW2", DB[a], 64 * a, 64 * a + 64, True, False, S2T[:3])
        for a in range(2):
            f, c = th(a)
            act(T.G2[:, f], T.SW2[:, 0:BWW].indirect(T.PL2[:, c]), S2T + ["PL2"], ["G2%d" % a])

    def L3v():
        f, c = th(2)
        cp(T.G2[:, f], T.SW2[:, 0:BWW].indirect(T.PL2[:, c]), S2T + ["PL2"], ["G22"])

    def L3e():
        for a in range(3):
            ext("XS", "G2", DB[a], 64 * a, 64 * a + 64, False, True, ["G2%d" % a])

    def L3b():
        for a in range(3):
            cp(T.DI[:, th(a)[1]], T[DB[a]][:, th(a)[1]], [DB[a]], (), ["DI"])

    def L3c():
        ts(T.DL[:], T.DI[:], 2047, A.bitwise_and, ["DI"], ["DL"])
        cp(T.DU[:], T.DL[:], ["DL"], ["DU"])

    def beaten():
        def counts(c0, c1, bt):
            for c in range(c0, c1):
                mm(T.ps2[:, 8 * c:8 * c + 8], T.bits[:, sl(c)], T.BD[:, 0::16], True, True, [bt, "BD"], (), ["ps2"])

        def vec(l, h, t):
            tt(T.bits[:, l:h], T.SWIN[:, 0:W].indirect(T.DU[:, l // 16:h // 16]), T.XW[:, l:h], A.is_le, ["S", "DU", "XWx"], [t])
            counts(l // 128, h // 128, t)

        act(T.SG[:], T.SWIN[:, 0:W].indirect(T.DU[:, 160:192]), ["S", "DU"], ["SG"])
        vec(0, 1024, "bits0")
        mm(T.ps7[:, :], T.ID[:], T.XW[:, 2560:3072], True, False, ["ID", "XWx"], ["ps7"])
        mm(T.ps7[:, :], T.NI[:], T.SG[:], False, True, ["NI", "SG"], (), ["ps7"])
        act(T.bits[:, 2560:3072], T.ps7[:, :], ["ps7"], ["bits3"], f=F.Sign, bias=TINY)
        vec(1024, 2048, "bits1")
        counts(20, 24, "bits3")
        vec(2048, 2560, "bits2")
        ts(T.bT[:, 0:160], T.ps2[:, 0:160], 4.5, A.is_lt, ["ps2"], ["bT"])
        ts(T.bT[:, 160:192], T.ps2[:, 160:192], -7.0, A.is_lt, ["ps2"], (), ["bT"])

    def ghosts_a():
        ts(T.dg2[:], T.DL[:], 31, A.bitwise_and, ["DL"], ["dg2"])
        ts(T.dg1[:], T.DL[:], 5, A.arith_shift_right, ["DL"], ["dg1"])
        cp(T.dlo[:], T.dg2[:], ["dg2"], ["dlo"])
        cp(T.dh[:], T.dg1[:], ["dg1"], ["dh"])
        dma(T.GW[10::16, :], T.dlo[:], ["dlo"], (), ["GW"])
        dma(T.GW[2::16, :], T.dh[:], ["dh"], (), ["GW"])

    def ghosts_b(t):
        act(T["GO%d" % t][:], T.GW[:].indirect(T.SL[:]), ["GW", "SL"], ["GO%d" % t])
        for d in range(1, N):
            send(T["GL%d" % t][:, sl(d - 1)], T["GO%d" % t][:, sl(d - 1)], cores[(r + d) % N], "gh%d" % t, ["GO%d" % t])
        arrive("gh%d" % t, sum(len(engs(cores[(r - d) % N], core)) for d in range(1, N)), "GL%d" % t)

    def ghosts_in(t):
        for b in ("BW", "SW1", "SW2"):
            dma(T[b][:, V:ROOT], T["GL%d" % t][:], ["GL%d" % t], [b + "g"])

    NS = 7
    vU = u_(4, 16)
    DUm = lambda nj: u_(3, nj)

    def compact(t):
        mm(T.ps3[:, 0:192], T.M1[:], T.bT[:], True, False, ["M1", "bT"], ["ps3"])
        for c in range(8):
            op("v", lambda q, c=c: q.tensor_tensor_scan(T.binc[:, c::8], T.ONE[:, c:192:8], T.bT[:, c::8], 0.0, A.mult, A.add),
               ["ONE", "bT"], (), ["binc"])
        mm(T.ps3[:, 0:192], T.ONE[:, 0:128], T.binc[:], False, True, ["ONE", "binc"], (), ["ps3"])
        mm(T.ps4[:, 0:1], T.binc[:, 0:128], T.ONE[:, 0:1], True, True, ["binc", "ONE"], ["ps4"])
        mm(T.ps4[0:64, 1:2], T.binc[:, 128:192], T.ONE[:, 0:1], True, True, ["binc", "ONE"], (), ["ps4"])
        ts(T.posI[:], T.ps3[:, 0:192], 4095.0, A.add, ["ps3"], ["posI"])
        ts(T.indA[:], T.krow[:], T.ps4[:, 0:1], A.is_ge, ["krow", "ps4"], ["indA"])
        ts(T.loI[:], T.posI[:], 15, A.bitwise_and, ["posI"], ["loI"])
        ts(T.hiI[:], T.posI[:], 4, A.arith_shift_right, ["posI"], ["hiI"])
        ts(T.indB[0:64, :], T.krow[0:64, :], T.ps4[0:64, 1:2], A.is_ge, ["krow", "ps4"], ["indB"])
        cp(T.lob[:], T.loI[:], ["loI"], ["lob"])
        cp(T.hib[:], T.hiI[:], ["hiI"], ["hib"])
        for i in range(16):
            mm(T.ps6[:, 0:16], T.SA[:, sl(i)], T.indA[:, i::16], i == 0, False, ["SA", "indA"], (), ["ps6"])
        for i in range(16):
            mm(T.ps6[:, 0:16], T.SA[0:64, sl(i)], T.indB[0:64, i::16], False, i == 15, ["SA", "indB"], (), ["ps6"])
        for i in range(NS):
            act(T.sq[:], T.lob[:], ["lob"], ["sq"], f=F.Square, bias=-float(i))
            act(T.OHL[:, i::16], T.sq[:], ["sq"], (), ["OHL"], f=F.Relu, scale=-1.0, bias=1.0)
        for i in range(NS, 16):
            ts(T.OHL[:, i::16], T.lob[:], float(i), A.is_equal, ["lob"], (), ["OHL"])
        for i in range(16):
            ts(T.OHH[:, i::16], T.hib[:], float(i), A.is_equal, ["hib", "c0"], (), ["OHH"], s2=col(0), op1=A.mult)
        for c in range(24):
            mm(T.ps5[:, 0:128], T.OHL[:, sl(c)], T.OHH[:, sl(c)], c == 0, c == 23, ["OHL", "OHH"], (), ["ps5"])
        if t < RO - 1:
            ghosts_a()
        if t == 0:
            consts5()
        o = lambda a, b: T.ov[:, a:b]
        tt(o(0, 128), T.ps5[:, 0:128], T.BD[:], A.mult, ["ps5", "BD"], ["ovm"])
        tt(o(128, 192), o(0, 64), o(64, 128), A.add, ["ovm"], ["ov1"])
        tt(o(192, 224), o(128, 160), o(160, 192), A.add, ["ov1"], ["ov2"])
        tt(o(224, 240), o(192, 208), o(208, 224), A.add, ["ov2"], ["ov3"])
        tt(T.vf[:], T.ps6[:, 0:16], o(224, 240), A.add, ["ps6", "ov3"], ["vf"])
        cp(vU, T.vf[:], ["vf"], ["vU"])

    def own_data():
        act(T.G2g[:], T.G2[:].indirect(vU), ["G20", "G21", "G22", "G2p", "vU", "c15"], ["G2g"], f=F.Identity, bias=col(15))
        cp(T.xB[:], T.XW[:].indirect(vU), ["XWx", "XWp", "vU"], ["xB"])
        tt(T.Dg[:], T.SW2[:, 0:BWW].indirect(vU), T.G2g[:], A.add, S2T + ["G2g", "vU"], ["Dg"])

    def spread(x, xt, XX, n, ks, e):
        for k in ks:
            if e == "v":
                cp(T[XX][:, k:16 * n:16], x, [xt], (), [XX])
            else:
                act(T[XX][:, k:16 * n:16], x, [xt], (), [XX])

    LB = {16: "ps6", 6: "ps4"}

    def choose_a(Dg, dt_, nj):
        for i in range(16):
            mm(T[LB[nj]][:, 0:nj], T.XS[:, sl(i)], Dg[:, i::16], i == 0, i == 15, ["XS", dt_], (), [LB[nj]])
        mm(T.ps7[:, 0:16 * nj], T.CB[:], Dg, True, False, ["CB", dt_], ["ps7"])

    def choose_b(nj):
        n = 16 * nj
        ts(n_(4, nj), T[LB[nj]][:, 0:nj], 8064.0, A.add, [LB[nj]], ["di"])
        ts(n_(5, nj), n_(4, nj), 2047, A.bitwise_and, ["di"], ["dm"])
        cp(DUm(nj), n_(5, nj), ["dm"], ["DUm"])
        cp(T.wkg[:, 0:n], T.WK[:].indirect(DUm(nj)), ["WK", "DUm"], ["wkg"])
        mm(T.ps7[:, 0:n], T.I7[:], T.wkg[:, 0:n], False, True, ["I7", "wkg"], (), ["ps7"])

    def choose_c(nj):
        n = 16 * nj
        ts(T.ci[:, 0:n], T.ps7[:, 0:n], 8064.0, A.add, ["ps7"], ["ci"])
        ts(T.cm[:, 0:n], T.ci[:, 0:n], 2047, A.bitwise_and, ["ci"], ["cm"])
        cp(T.cu[:, 0:n], T.cm[:, 0:n], ["cm"], ["cu"])

    def choose_d(XX, nj, parts):
        n = 16 * nj
        mm(T.ps2[:, 0:n], T.ID[:], T.KC[:, 0:n], True, False, ["ID", "KC"], ["ps2"])
        for j0, j1 in parts:
            for j in range(j0, j1):
                tt(T.B2[:, j, :], T.SWIN[:, 0:W].indirect(T.cu[:, 16 * j:16 * j + 16]), T[XX][:, 256 * j:256 * j + 256], A.is_lt,
                   ["S", "cu", XX], ["B2%d" % j])
            for i in range(16):
                mm(T.ps2[:, 16 * j0:16 * j1], T.XE[:, sl(i)], T.B2[:, j0:j1, 16 * i:16 * i + 16], False, False,
                   ["XE"] + ["B2%d" % j for j in range(j0, j1)], (), ["ps2"])
        cp(T.ctc[:, 0:nj, 0:16], T.cm[:, 0:n], ["cm"], (), ["ctc"])
        cp(T.ctc[:, 0:nj, 16:32], T.cm[:, 0:n], ["cm"], (), ["ctc"])
        op("v", lambda q: q.transpose(T.ctt[:, 0:nj, :], T.ctc[:, 0:nj, :]), ["ctc"], ["ctt"])
        mm(T.ps2[:, 0:n], T.Ie[:], T.ctt[:, 0:nj, 0:16], False, False, ["Ie", "ctt"], (), ["ps2"])
        mm(T.ps2[:, 0:n], T.Io[:], T.ctt[:, 0:nj, 16:32], False, True, ["Io", "ctt"], (), ["ps2"])

    def choose_e(nj):
        n = 16 * nj
        K = T.key
        cp(K[:, 0:n], T.ps2[:, 0:n], ["ps2"], ["key0"])
        tt(K[:, 256:256 + n // 2], K[:, 0:n:2], K[:, 1:n:2], A.max, ["key0"], ["key1"])
        tt(K[:, 384:384 + n // 4], K[:, 256:256 + n // 2:2], K[:, 257:256 + n // 2:2], A.max, ["key1"], ["key2"])
        tt(K[:, 448:448 + n // 8], K[:, 384:384 + n // 4:2], K[:, 385:384 + n // 4:2], A.max, ["key2"], ["key3"])
        tt(K[:, 480:480 + nj], K[:, 448:448 + n // 8:2], K[:, 449:448 + n // 8:2], A.max, ["key3"], ["kmax"])

    def moved(t, nj):
        km = T.key[:, 480:480 + nj]
        ts(f_(0, nj), km, T.thr[:, t:t + 1], A.is_ge, ["kmax", "thr%d" % t], ["mv"])
        ts(n_(0, nj), km, 2047, A.bitwise_and, ["kmax"], ["c1i"])

    def early():
        tt(f_(14, 16), T.vf[:], tr(1, 16), A.subtract, ["vf", "trP"], ["vt"])
        ts(f_(15, 16), T.vf[:], 3071.5, A.is_lt, ["vf"], ["val"])

    def move_list():
        km = T.key[:, 480:496]
        ts(n_(3, 16), km, 31, A.bitwise_and, ["kmax"], ["c4i"])
        ts(n_(2, 16), km, 5, A.arith_shift_right, ["kmax"], ["c3i"], s2=63, op1=A.bitwise_and)
        cp(b_(1, 16), n_(3, 16), ["c4i"], ["lb"])
        cp(b_(0, 16), n_(2, 16), ["c3i"], ["hb"])
        for i in range(16):
            mm(T.ps3[:, i:256:16], T.XLh[:, sl(i)], b_(0, 16), True, False, ["XLh", "hb"], (), ["ps3"])
            mm(T.ps3[:, i:256:16], T.XLl[:, sl(i)], b_(1, 16), False, True, ["XLl", "lb"], (), ["ps3"])
        act(T.RD[:], T.ps3[:, 0:256], ["ps3", "c5"], ["RD"], f=F.Identity, bias=col(5))
        tt(f_(2, 16), f_(0, 16), f_(14, 16), A.mult, ["mv", "vt"], ["m1"])
        tt(u_(0, 16), f_(2, 16), tr(1, 16), A.add, ["m1", "trP"], ["voff"])

    def move_put(last):
        cp(T.BW[:, 0:4240].indirect(u_(0, 16)), T.RD[:], ["RD", "voff"], BWT)
        if not last:
            keep()

    def refuse_a():
        tt(b_(2, 16), f_(15, 16), f_(0, 16), A.subtract, ["val", "mv"], ["rf"])
        op("v", lambda q: q.tensor_tensor_scan(b_(3, 16), T.ONE[:, 0:16], b_(2, 16), 0.0, A.mult, A.add), ["ONE", "rf"], ["finc"])
        mm(T.ps4[:, 0:16], T.M1g[:], b_(2, 16), True, False, ["M1g", "rf"], ["ps4"])
        mm(T.ps4[:, 0:16], T.BD[:], b_(3, 16), False, True, ["BD", "finc"], (), ["ps4"])

    def refuse_b():
        ts(f_(3, 16), T.ps4[:, 0:16], 4095.0, A.add, ["ps4"], ["rq"])
        ts(f_(4, 16), f_(3, 16), 95.5, A.is_lt, ["rq"], ["rs"])
        tt(f_(5, 16), f_(3, 16), tr(3, 16), A.subtract, ["rq", "trR"], ["rt"])
        tt(f_(6, 16), f_(4, 16), f_(5, 16), A.mult, ["rs", "rt"], ["rr"])
        tt(u_(1, 16), f_(6, 16), tr(3, 16), A.add, ["rr", "trR"], ["roff"])

    def refuse_c(t):
        G = T["GS%d" % t]
        ga, gb = "GSa%d" % t, "GSb%d" % t
        cp(G[:, 0:448].indirect(u_(1, 16)), T.xB[:], ["xB", "roff"], [ga, gb])
        cp(G[:, 96:544].indirect(u_(1, 16)), T.Dg[:], ["Dg", "roff", ga], [gb])
        dst, src = cores[(r + 1 + t % (N - 1)) % N], cores[(r - 1 - t % (N - 1)) % N]
        send(T["GX%d" % t][:], G[:, 0:192], dst, "gu%d" % t, [ga, gb])
        arrive("gu%d" % t, len(engs(src, core)), "GX%d" % t)

    def parity_a():
        op("v", lambda q: q.tensor_reduce(f_(7, 1), f_(0, 16), AxisListType.X, A.add), ["mv"], ["mr"])
        cp(b_(4, 1), f_(7, 1), ["mr"], ["mrb"])
        mm(T.ps4[:, 16:17], T.ONE[:, 0:128], b_(4, 1), True, True, ["ONE", "mrb"], (), ["ps4"])

    def parity_b(t):
        cp(n_(1, 1), T.ps4[:, 16:17], ["ps4"], ["pi"])
        ts(n_(1, 1), n_(1, 1), 1, A.bitwise_and, ["pi"], ["pi"])
        ts(T.thr[:, t + 1:t + 2], n_(1, 1), SC, A.mult, ["pi"], ["thr%d" % (t + 1)], s2=9 * SC, op1=A.add)

    def dedup_a(nj):
        ts(f_(8, nj), n_(0, nj), 1.0, A.add, ["c1i"], ["cp1"])
        tt(f_(10, nj), n_(0, nj), tr(2, nj), A.subtract, ["c1i", "trS"], ["ct2"])
        tt(f_(9, nj), f_(8, nj), f_(0, nj), A.mult, ["cp1", "mv"], ["cmf"])
        cp(T.cmh[:, 0:nj], f_(9, nj), ["cmf"], ["cmh"])
        for i in range(16):
            mm(T.ps5[:, i:16 * nj:16], T.XA[:, sl(i)], T.cmh[:, 0:nj], True, True, ["XA", "cmh"], (), ["ps5"])

    def dedup_b(nj):
        n = 16 * nj
        cp(T.cR[:, 0:n], T.ps5[:, 0:n], ["ps5"], ["cR"])
        mm(T.ps5[:, 0:n], T.BD[:], T.ZER[:, 0:n], True, False, ["BD", "ZER"], ["ps5"])
        for j in range(nj):
            ts(T.DE[:, j, 0:n - 16 * j], T.cR[:, 16 * j:n], T.sml[:, 144 + j:145 + j], A.is_equal, ["cR", "cmf"], ["DE%d" % j])
            if j < nj - 1:
                mm(T.ps5[:, 16 * (j + 1):n], T.BD[:], T.DE[:, j, 16:n - 16 * j], False, False, ["BD", "DE%d" % j], (), ["ps5"])
        tt(T.DMb[:, 0:nj, :], T.DE[:, 0:nj, 0:16], T.MK[:, 0:nj, :], A.mult, ["DE%d" % j for j in range(nj)] + ["MK"], ["DMb"])
        mm(T.ps5[:, 0:n], T.BD[:], T.DMb[:, 0:nj, :], False, True, ["BD", "DMb"], (), ["ps5"])

    def dedup_c(nj):
        n = 16 * nj
        cp(T.dupR[:, 0:n], T.ps5[:, 0:n], ["ps5"], ["dupR"])
        for i in range(16):
            mm(T.ps6[:, 16:16 + nj], T.XE[:, sl(i)], T.dupR[:, i:n:16], i == 0, i == 15, ["XE", "dupR"], (), ["ps6"])

    def dedup_d(nj, x, xt):
        ts(f_(11, nj), T.ps6[:, 16:16 + nj], 0.5, A.is_lt, ["ps6"], ["nd"])
        tt(f_(12, nj), f_(11, nj), f_(0, nj), A.mult, ["nd", "mv"], ["fm"])
        tt(f_(13, nj), f_(12, nj), f_(10, nj), A.mult, ["fm", "ct2"], ["fq"])
        tt(u_(2, nj), f_(13, nj), tr(2, nj), A.add, ["fq", "trS"], ["soff"])
        cp(T.SWIN[:, 0:2304].indirect(u_(2, nj)), x, [xt, "soff"], ["S"])

    for t in range(RO):
        last = t == RO - 1
        if t:
            gx, gt = T["GX%d" % (t - 1)], "GX%d" % (t - 1)
            ghosts_in(t - 1)
            ext("XP", "BW", "ps0", 0, 192, True, True, ["BW"])
            dedup_b(16)
            anchors("PL")
        dbl(1, 0)
        if t:
            dedup_c(16)
        dbl(1, 1); dbl(1, 2)
        if t:
            dedup_d(16, T.xB[:], "xB")
        anchors("PL1")
        if t:
            spread(gx[:, 0:96], gt, "XXg", Q, range(16), "s")
            choose_a(gx[:, 96:192], gt, 6)
        dbl(2, 0)
        if t == 0:
            fill("SA", "BA", [], 1.0)
        else:
            choose_b(6)
        dbl(2, 1); dbl(2, 2)
        if t:
            choose_c(6)
        anchors("PL2")
        L3a()
        if t == 0:
            consts3()
            fill("XE", "BG", [], SC)
            L3v()
        else:
            choose_d("XXg", 6, [(0, 6)])
            L3v()
            choose_e(6); moved(t - 1, 6); dedup_a(6)
        L3e()
        if t:
            dedup_b(6)
        L3b()
        if t:
            dedup_c(6)
        L3c()
        if t:
            dedup_d(6, gx[:, 0:96], gt)
        beaten()
        compact(t)
        own_data()
        spread(T.xB[:], "xB", "XX", 256, range(0, 9), "s")
        choose_a(T.Dg[:], "Dg", 16)
        spread(T.xB[:], "xB", "XX", 256, range(9, 16), "v")
        early()
        choose_b(16)
        if not last:
            ghosts_b(t)
        choose_c(16)
        choose_d("XX", 16, [(0, 4), (4, 8), (8, 12), (12, 16)])
        choose_e(16)
        moved(t, 16)
        refuse_a()
        if last:
            dedup_a(16)
            refuse_b(); refuse_c(t)
        else:
            move_list()
            refuse_b()
            dedup_a(16)
            parity_a()
            refuse_c(t)
            move_put(False)
            parity_b(t)
    gx, gt = T.GX2, "GX2"
    dedup_b(16); dedup_c(16)
    choose_a(gx[:, 96:192], gt, 6)
    spread(gx[:, 0:96], gt, "XXg", Q, range(16), "s")
    dedup_d(16, T.xB[:], "xB")
    choose_b(6); choose_c(6)
    move_list()
    choose_d("XXg", 6, [(0, 6)])
    move_put(True)
    choose_e(6); moved(2, 6); dedup_a(6)

    def outs(b):
        p = ["ps0", "ps1", "ps3"][b % 3]
        mm(T[p][0:40, :], T.OC[:], T.BW[:, 512 * b:512 * b + 512], True, True, ["OC", "BW"], [p])
        act(T.OUT[:, 512 * b:512 * b + 512], T[p][0:40, :], [p], (), ["OUT"])

    dedup_b(6)
    for b in range(2):
        outs(b)
    dedup_c(6); dedup_d(6, gx[:, 0:96], gt)
    for b in range(2, 6):
        outs(b)
    dma(T.yan[:], T.OUT[0:8, :], ["OUT"])
    dma(T.yof[:], T.OUT[32:40, :], ["OUT"])
    dma(T.ys[:], T.SWIN[:, 0:W], ["S"])
    for s in total:
        g.wait_ge(T.sem[s], total[s])
